import numpy as np
import ml_dtypes


def mxq(x, axis, fmt="e4m3"):
    dtype, down = {"e4m3": (ml_dtypes.float8_e4m3fn, 7), "e5m2": (ml_dtypes.float8_e5m2, 14)}[fmt]
    v = np.moveaxis(np.asarray(x, np.float32).astype(ml_dtypes.bfloat16).astype(np.float64), axis, -1)
    blocks = v.reshape(v.shape[:-1] + (-1, 32))
    amax = np.abs(blocks).max(-1, keepdims=True)
    byte = np.maximum(np.where(amax > 0, np.frexp(amax)[1] - 1 + 127, 0) - down, 1)
    scale = np.exp2(byte - 127.0)
    codes = (blocks / scale).astype(np.float32).astype(dtype).astype(np.float64)
    return np.moveaxis((codes * scale).reshape(v.shape), -1, axis)


WIDE = False


def mx_kscale(k):
    if not WIDE:
        return np.ones(k)
    levels = np.array([10, -10, 5, -5, 0])
    if k % 512:
        return np.exp2(np.random.permutation(np.resize(levels, k // 32))).repeat(32)
    a = np.empty((k // 512, 16))
    for p in range(k // 512):
        a[p, :8] = np.random.permutation(np.resize(levels, 8))
        for g in range(8):
            far = levels[np.abs(levels - a[p, g]) >= 10]
            a[p, g + 8] = far[np.random.randint(len(far))]
    return np.exp2(a.ravel()).repeat(32)


def f64(x):
    return np.asarray(x).astype(np.float64)


def striped(idx):
    return np.tile(idx.reshape(-1, 16).T, (8, 1)).astype(np.uint16)


def unstriped(offs):
    return offs[:16].T.reshape(-1).astype(np.int64)


E2M1 = np.array([0.0, 0.5, 1.0, 1.5, 2.0, 3.0, 4.0, 6.0, -0.0, -0.5, -1.0, -1.5, -2.0, -3.0, -4.0, -6.0])


def pack_weight(w, fmt):
    k, n = w.shape
    w = f64(np.asarray(w, np.float32).astype(ml_dtypes.bfloat16)).reshape(k // 32, 32, n)
    amax = np.abs(w).max(1)
    if fmt == "e4m3":
        byte = np.frexp(amax)[1] - 1 + 127 - 7
    else:
        mant, ex = np.frexp(amax / 6.0)
        byte = np.where(mant > 0.5, ex, ex - 1) + 127
    byte = np.clip(np.where(amax > 0, byte, 1), 1, 254)
    scaled = (w * np.exp2(127.0 - byte)[:, None, :]).reshape(k, n).astype(np.float32)
    by_word = np.ascontiguousarray(scaled.reshape(k // 512, 128, 4, n).transpose(0, 1, 3, 2))
    if fmt == "e4m3":
        words = by_word.astype(ml_dtypes.float8_e4m3fn).view(np.uint8)
    else:
        c = by_word.astype(ml_dtypes.float4_e2m1fn).view(np.uint8) & 0xF
        words = (c[..., 0::2] | (c[..., 1::2] << 4)).reshape(k // 512, 128, 2 * n)
    return np.ascontiguousarray(words), np.ascontiguousarray(byte.astype(np.uint8).reshape(k // 512, 16, n))


def unpack_weight(words, scales, fmt):
    g, _, n = scales.shape
    words = np.ascontiguousarray(words).reshape(g, 128, n, -1)
    if fmt == "e4m3":
        vals = words.view(ml_dtypes.float8_e4m3fn).astype(np.float64)
    else:
        nib = np.empty((g, 128, n, 4), np.uint8)
        nib[..., 0::2] = words & 0xF
        nib[..., 1::2] = words >> 4
        vals = E2M1[nib]
    vals = vals * np.repeat(np.exp2(scales.astype(np.float64) - 127.0), 8, axis=1)[..., None]
    return vals.transpose(0, 1, 3, 2).reshape(g * 512, n)


def pack_table(v):
    words, scales = pack_weight(v, "e4m3")
    return np.concatenate([words.reshape(words.shape[0], -1), scales.reshape(scales.shape[0], -1)], axis=1)


def unpack_table(tab):
    g, t = tab.shape[0], tab.shape[1] // 528
    return unpack_weight(tab[:, :512 * t].reshape(g, 128, t, 4), tab[:, 512 * t:].reshape(g, 16, t), "e4m3")


K, R, M, T, S = 1536, 512, 1024, 1024, 256


def setup_inputs():
    n = np.random.standard_normal
    s = mx_kscale(K)[:, None]
    u = mx_kscale(R)[:, None]
    p_w4 = pack_weight(n((K, M)) / np.sqrt(K) / s, "e2m1")
    return {
        "tab": pack_table(n((K, T)) * s),
        "w4_words": p_w4[0],
        "w4_scales": p_w4[1],
        "down": (n((K, R)) / np.sqrt(K) / s * u.T).astype(np.float32),
        "up": (0.5 * n((R, M)) / np.sqrt(R) / u).astype(np.float32),
        "offs": striped(np.random.permutation(T)[:S]),
    }


def reference(tab, w4_words, w4_scales, down, up, offs):
    tab_ = unpack_table(tab)[:, unstriped(offs)]
    w4_ = unpack_weight(w4_words, w4_scales, "e2m1")
    down_ = mxq(f64(down), 0, "e4m3")
    up_ = mxq(f64(up), 0, "e4m3")
    h_ = mxq(down_.T @ tab_, 0, "e4m3")
    y = tab_.T @ w4_ + h_.T @ up_
    return y

@@ -1,0 +1,219 @@
+from contextlib import ExitStack
+
+import concourse.mybir as mybir
+
+K, R, M, T, S = 1536, 512, 1024, 1024, 256
+FLOPS = 2 * S * (K * R + K * M + R * M)
+
+F32 = mybir.dt.float32
+BF16 = mybir.dt.bfloat16
+I32 = mybir.dt.int32
+U32 = mybir.dt.uint32
+U16 = mybir.dt.uint16
+U8 = mybir.dt.uint8
+FP8X4 = mybir.dt.float8_e4m3fn_x4
+FP4X4 = mybir.dt.float4_e2m1fn_x4
+
+P = 128
+PASSES = K // 512
+N_TILE = 512
+U_STARTS = (0, 256, 512, 768)
+U_WIDTHS = (256, 256, 256, 256)
+U_VECTOR = (256, 0, 0, 256)
+CHUNKS = len(U_STARTS)
+WORD_COLS = 512 * T // 4
+
+
+def tile_list_tablora_tm_none_kernel(tc, tab, w4_words, w4_scales, down, up, offs, out):
+    nc = tc.nc
+    with ExitStack() as ctx:
+        keep = ctx.enter_context(tc.tile_pool(name="keep", bufs=1))
+        psum = ctx.enter_context(tc.psum_pool(name="psum", bufs=1))
+
+        offsets = keep.tile([P, S // 16], U16, name="offsets")
+        words = [keep.tile([P, T], I32, name=f"words{a}", align_bytes=64) for a in range(PASSES)]
+        tab_plane = keep.tile([P, PASSES * T // 4], I32, name="tab_plane", align_bytes=64)
+        w4_plane = keep.tile([P, PASSES * M // 4], I32, name="w4_plane", align_bytes=64)
+        w4 = keep.tile([P, PASSES, 2 * M], U8, name="w4", align_bytes=64)
+        d_raw = [keep.tile([P, 4, R], F32, name=f"d_raw{a}", align_bytes=64) for a in range(PASSES)]
+        d_grp = [keep.tile([P, 4, P, 4], BF16, name=f"d_grp{a}", align_bytes=64) for a in range(PASSES)]
+        d_codes = [keep.tile([P, R], U32, name=f"d_codes{a}", align_bytes=64) for a in range(PASSES)]
+        d_scales = [keep.tile([P, R], U8, name=f"d_scales{a}", align_bytes=64) for a in range(PASSES)]
+        u_raw = [keep.tile([P, 4, U_WIDTHS[c]], F32, name=f"u_raw{c}", align_bytes=64) for c in range(CHUNKS)]
+        u_grp = [keep.tile([P, N_TILE, 4], BF16, name=f"u_grp{n}", align_bytes=64) for n in range(2)]
+        u_codes = [keep.tile([P, N_TILE], U32, name=f"u_codes{n}", align_bytes=64) for n in range(2)]
+        u_scales = [keep.tile([P, N_TILE], U8, name=f"u_scales{n}", align_bytes=64) for n in range(2)]
+        v_codes = [keep.tile([P, S], U32, name=f"v_codes{a}", align_bytes=64) for a in range(PASSES)]
+        v_scales = [keep.tile([P, S], U8, name=f"v_scales{a}", align_bytes=64) for a in range(PASSES)]
+        h_raw = keep.tile([P, 4, S], BF16, name="h_raw", align_bytes=64)
+        h_grp = keep.tile([P, S, 4], BF16, name="h_grp", align_bytes=64)
+        h_codes = keep.tile([P, S], U32, name="h_codes", align_bytes=64)
+        h_scales = keep.tile([P, S], U8, name="h_scales", align_bytes=64)
+        o_sb = [[keep.tile([P, N_TILE], F32, name=f"o_sb{j}{n}", align_bytes=64) for n in range(2)] for j in range(2)]
+        h_ps = [psum.tile([P, S], F32, name=f"h_ps{t}") for t in range(4)]
+        o_ps = [[psum.tile([P, N_TILE], F32, name=f"o_ps{j}{n}") for n in range(2)] for j in range(2)]
+
+        nc.vector.memset(tab_plane[:], 0)
+        nc.vector.memset(w4_plane[:], 0)
+        nc.sync.dma_start(offsets[:], offs)
+        tab_i = tab.bitcast(I32)
+        tab_s = tab_i[:, WORD_COLS:].rearrange("a (q r t) -> r q a t", q=4, r=4)
+        w4_s = w4_scales.bitcast(I32).rearrange("a (q r) n -> r q a n", q=4, r=4)
+        def load_words(a):
+            nc.sync.dma_start(out=words[a][:], in_=tab_i[a, :WORD_COLS].rearrange("(p t) -> p t", p=P))
+
+        def load_down(a):
+            nc.sync.dma_start(
+                out=d_raw[a][:], in_=down[512 * a : 512 * (a + 1), :].rearrange("(p j) r -> p j r", j=4)
+            )
+
+        def load_scales(plane, rows):
+            for r in range(4):
+                nc.sync.dma_start(out=plane[r:P:32, :].rearrange("q (a t) -> q a t", a=PASSES), in_=rows[r])
+
+        load_down(0)
+        load_scales(tab_plane, tab_s)
+        load_down(1)
+        load_words(0)
+        load_words(1)
+        load_down(2)
+        load_scales(w4_plane, w4_s)
+        nc.sync.dma_start(out=w4[:].bitcast(I32), in_=w4_words.bitcast(I32).rearrange("a p n -> p a n"))
+        load_words(2)
+        up_v = up.rearrange("(p j) n -> p j n", j=4)
+        for c in range(CHUNKS):
+            nc.sync.dma_start(out=u_raw[c][:], in_=up_v[:, :, U_STARTS[c] : U_STARTS[c] + U_WIDTHS[c]])
+
+        tab_bytes = tab_plane[:].bitcast(U8)
+        w4_bytes = w4_plane[:].bitcast(U8)
+
+        def gather_words(a):
+            nc.vector.tensor_copy(v_codes[a][:], words[a][:].bitcast(U32).indirect(offsets[:]))
+
+        def gather_scales(a):
+            nc.vector.tensor_copy(v_scales[a][:], tab_bytes[:, a * T : (a + 1) * T].indirect(offsets[:]))
+
+        def group_down(a):
+            src = d_raw[a][:].rearrange("p j (m t) -> p m j t", t=4)
+            dst = d_grp[a][:].rearrange("p t m j -> p m j t")
+            if a < 2:
+                nc.scalar.copy(out=dst, in_=src)
+            else:
+                nc.vector.tensor_copy(out=dst, in_=src)
+
+        def quantize_down(a):
+            nc.vector.quantize_mx(
+                out=d_codes[a][:].bitcast(FP8X4),
+                scales=d_scales[a][:],
+                in_=d_grp[a][:].rearrange("p t m j -> p (t m j)"),
+            )
+
+        def prepare_up(c):
+            n, first, width, v = U_STARTS[c] // N_TILE, U_STARTS[c] % N_TILE, U_WIDTHS[c], U_VECTOR[c]
+            src = u_raw[c][:].rearrange("p j (c i) -> p c j i", i=4)
+            dst = u_grp[n][:, first : first + width, :].rearrange("p (c i) j -> p c j i", i=4)
+            if v > 0:
+                nc.vector.tensor_copy(out=dst[:, 0 : v // 4], in_=src[:, 0 : v // 4])
+            if v < width:
+                nc.scalar.copy(out=dst[:, v // 4 : width // 4], in_=src[:, v // 4 : width // 4])
+            cols = slice(first, first + width)
+            nc.vector.quantize_mx(
+                out=u_codes[n][:, cols].bitcast(FP8X4),
+                scales=u_scales[n][:, cols],
+                in_=u_grp[n][:, cols, :].rearrange("p w j -> p (w j)"),
+            )
+
+        def base(a, n):
+            for j in range(2):
+                js = slice(P * j, P * (j + 1))
+                nc.tensor.matmul_mx(
+                    out=o_ps[j][n][:],
+                    lhsT=v_codes[a][:, js].bitcast(FP8X4),
+                    lhsT_scale=v_scales[a][:, js],
+                    rhs=w4[:, a, 1024 * n : 1024 * (n + 1)].bitcast(FP4X4),
+                    rhs_scale=w4_bytes[:, a * M + N_TILE * n : a * M + N_TILE * (n + 1)],
+                    start=(a == 0),
+                    stop=False,
+                )
+
+        def low_rank(a):
+            for t in range(4):
+                ts = slice(P * t, P * (t + 1))
+                nc.tensor.matmul_mx(
+                    out=h_ps[t][:],
+                    lhsT=d_codes[a][:, ts].bitcast(FP8X4),
+                    lhsT_scale=d_scales[a][:, ts],
+                    rhs=v_codes[a][:].bitcast(FP8X4),
+                    rhs_scale=v_scales[a][:],
+                    start=(a == 0),
+                    stop=(a == PASSES - 1),
+                )
+
+        def close(c):
+            n, first, width = U_STARTS[c] // N_TILE, U_STARTS[c] % N_TILE, U_WIDTHS[c]
+            cols = slice(first, first + width)
+            for j in range(2):
+                nc.tensor.matmul_mx(
+                    out=o_ps[j][n][:, cols],
+                    lhsT=h_codes[:, P * j : P * (j + 1)].bitcast(FP8X4),
+                    lhsT_scale=h_scales[:, P * j : P * (j + 1)],
+                    rhs=u_codes[n][:, cols].bitcast(FP8X4),
+                    rhs_scale=u_scales[n][:, cols],
+                    start=False,
+                    stop=(first + width == N_TILE),
+                )
+
+        def store(n, first, width):
+            cols = slice(first, first + width)
+            for j in range(2):
+                if j == 0 and n == 1:
+                    nc.vector.tensor_copy(out=o_sb[j][n][:, cols], in_=o_ps[j][n][:, cols])
+                else:
+                    nc.scalar.copy(out=o_sb[j][n][:, cols], in_=o_ps[j][n][:, cols])
+                nc.sync.dma_start(
+                    out=out[P * j : P * (j + 1), N_TILE * n + first : N_TILE * n + first + width],
+                    in_=o_sb[j][n][:, cols],
+                )
+
+        group_down(0)
+        for a in range(PASSES):
+            gather_scales(a)
+        group_down(1)
+        quantize_down(0)
+        gather_words(0)
+        low_rank(0)
+        quantize_down(1)
+        gather_words(1)
+        low_rank(1)
+        group_down(2)
+        quantize_down(2)
+        for a in range(2):
+            for n in range(2):
+                base(a, n)
+        gather_words(2)
+        low_rank(2)
+        base(2, 0)
+        base(2, 1)
+        for t in range(4):
+            if t < 2:
+                nc.vector.tensor_copy(out=h_raw[:, t, :], in_=h_ps[t][:])
+            else:
+                nc.scalar.copy(out=h_raw[:, t, :], in_=h_ps[t][:])
+        nc.vector.tensor_copy(
+            out=h_grp[:].rearrange("p (c i) t -> p c t i", i=8),
+            in_=h_raw[:].rearrange("p t (c i) -> p c t i", i=8),
+        )
+        nc.vector.quantize_mx(
+            out=h_codes[:].bitcast(FP8X4), scales=h_scales[:], in_=h_grp[:].rearrange("p w j -> p (w j)")
+        )
+        prepare_up(0)
+        prepare_up(1)
+        close(0)
+        close(1)
+        prepare_up(2)
+        store(0, 0, N_TILE)
+        close(2)
+        prepare_up(3)
+        close(3)
+        store(1, 0, N_TILE // 2)
+        store(1, N_TILE // 2, N_TILE // 2)

@@ -17,11 +17,10 @@ FP4X4 = mybir.dt.float4_e2m1fn_x4
 P = 128
 PASSES = K // 512
 N_TILE = 512
-U_STARTS = (0, 256, 512, 768)
-U_WIDTHS = (256, 256, 256, 256)
-U_VECTOR = (256, 0, 0, 256)
-CHUNKS = len(U_STARTS)
+CHUNK = 256
 WORD_COLS = 512 * T // 4
+D_SPLIT = 88
+U_SPLIT = 176
 
 
 def tile_list_tablora_tm_none_kernel(tc, tab, w4_words, w4_scales, down, up, offs, out):
@@ -34,23 +33,25 @@ def tile_list_tablora_tm_none_kernel(tc, tab, w4_words, w4_scales, down, up, off
         words = [keep.tile([P, T], I32, name=f"words{a}", align_bytes=64) for a in range(PASSES)]
         tab_plane = keep.tile([P, PASSES * T // 4], I32, name="tab_plane", align_bytes=64)
         w4_plane = keep.tile([P, PASSES * M // 4], I32, name="w4_plane", align_bytes=64)
-        w4 = keep.tile([P, PASSES, 2 * M], U8, name="w4", align_bytes=64)
+        w4_lo = keep.tile([P, PASSES, 2 * N_TILE], U8, name="w4_lo", align_bytes=64)
+        w4_hi = keep.tile([P, PASSES - 1, 2 * N_TILE], U8, name="w4_hi", align_bytes=64)
+        w4_last = keep.tile([P, 2 * N_TILE], U8, name="w4_last", align_bytes=64)
         d_raw = [keep.tile([P, 4, R], F32, name=f"d_raw{a}", align_bytes=64) for a in range(PASSES)]
         d_grp = [keep.tile([P, 4, P, 4], BF16, name=f"d_grp{a}", align_bytes=64) for a in range(PASSES)]
         d_codes = [keep.tile([P, R], U32, name=f"d_codes{a}", align_bytes=64) for a in range(PASSES)]
         d_scales = [keep.tile([P, R], U8, name=f"d_scales{a}", align_bytes=64) for a in range(PASSES)]
-        u_raw = [keep.tile([P, 4, U_WIDTHS[c]], F32, name=f"u_raw{c}", align_bytes=64) for c in range(CHUNKS)]
-        u_grp = [keep.tile([P, N_TILE, 4], BF16, name=f"u_grp{n}", align_bytes=64) for n in range(2)]
-        u_codes = [keep.tile([P, N_TILE], U32, name=f"u_codes{n}", align_bytes=64) for n in range(2)]
-        u_scales = [keep.tile([P, N_TILE], U8, name=f"u_scales{n}", align_bytes=64) for n in range(2)]
+        u_lo = keep.tile([P, 4, N_TILE], F32, name="u_lo", align_bytes=64)
+        u_hi = [keep.tile([P, 4, CHUNK], F32, name=f"u_hi{c}", align_bytes=64) for c in range(2)]
+        u_grp = [keep.tile([P, CHUNK, 4], BF16, name=f"u_grp{c}", align_bytes=64) for c in range(4)]
+        u_codes = [keep.tile([P, CHUNK], U32, name=f"u_codes{c}", align_bytes=64) for c in range(4)]
+        u_scales = [keep.tile([P, CHUNK], U8, name=f"u_scales{c}", align_bytes=64) for c in range(4)]
         v_codes = [keep.tile([P, S], U32, name=f"v_codes{a}", align_bytes=64) for a in range(PASSES)]
         v_scales = [keep.tile([P, S], U8, name=f"v_scales{a}", align_bytes=64) for a in range(PASSES)]
-        h_raw = keep.tile([P, 4, S], BF16, name="h_raw", align_bytes=64)
-        h_grp = keep.tile([P, S, 4], BF16, name="h_grp", align_bytes=64)
-        h_codes = keep.tile([P, S], U32, name="h_codes", align_bytes=64)
-        h_scales = keep.tile([P, S], U8, name="h_scales", align_bytes=64)
+        h_grp = [keep.tile([P, P, 4], BF16, name=f"h_grp{j}", align_bytes=64) for j in range(2)]
+        h_codes = [keep.tile([P, P], U32, name=f"h_codes{j}", align_bytes=64) for j in range(2)]
+        h_scales = [keep.tile([P, P], U8, name=f"h_scales{j}", align_bytes=64) for j in range(2)]
         o_sb = [[keep.tile([P, N_TILE], F32, name=f"o_sb{j}{n}", align_bytes=64) for n in range(2)] for j in range(2)]
-        h_ps = [psum.tile([P, S], F32, name=f"h_ps{t}") for t in range(4)]
+        h_ps = [psum.tile([P, 4, P], F32, name=f"h_ps{j}") for j in range(2)]
         o_ps = [[psum.tile([P, N_TILE], F32, name=f"o_ps{j}{n}") for n in range(2)] for j in range(2)]
 
         nc.vector.memset(tab_plane[:], 0)
@@ -59,6 +60,10 @@ def tile_list_tablora_tm_none_kernel(tc, tab, w4_words, w4_scales, down, up, off
         tab_i = tab.bitcast(I32)
         tab_s = tab_i[:, WORD_COLS:].rearrange("a (q r t) -> r q a t", q=4, r=4)
         w4_s = w4_scales.bitcast(I32).rearrange("a (q r) n -> r q a n", q=4, r=4)
+        w4_i = w4_words.bitcast(I32).rearrange("a p n -> p a n")
+        up_v = up.rearrange("(p j) n -> p j n", j=4)
+        half = N_TILE // 2
+
         def load_words(a):
             nc.sync.dma_start(out=words[a][:], in_=tab_i[a, :WORD_COLS].rearrange("(p t) -> p t", p=P))
 
@@ -73,16 +78,18 @@ def tile_list_tablora_tm_none_kernel(tc, tab, w4_words, w4_scales, down, up, off
 
         load_down(0)
         load_scales(tab_plane, tab_s)
-        load_down(1)
-        load_words(0)
-        load_words(1)
-        load_down(2)
         load_scales(w4_plane, w4_s)
-        nc.sync.dma_start(out=w4[:].bitcast(I32), in_=w4_words.bitcast(I32).rearrange("a p n -> p a n"))
+        load_words(0)
+        load_down(1)
+        load_down(2)
+        load_words(1)
         load_words(2)
-        up_v = up.rearrange("(p j) n -> p j n", j=4)
-        for c in range(CHUNKS):
-            nc.sync.dma_start(out=u_raw[c][:], in_=up_v[:, :, U_STARTS[c] : U_STARTS[c] + U_WIDTHS[c]])
+        nc.sync.dma_start(out=w4_lo[:].bitcast(I32), in_=w4_i[:, :, :half])
+        nc.sync.dma_start(out=u_lo[:], in_=up_v[:, :, :N_TILE])
+        nc.sync.dma_start(out=w4_hi[:].bitcast(I32), in_=w4_i[:, : PASSES - 1, half:])
+        for c in range(2):
+            nc.sync.dma_start(out=u_hi[c][:], in_=up_v[:, :, N_TILE + CHUNK * c : N_TILE + CHUNK * (c + 1)])
+        nc.sync.dma_start(out=w4_last[:].bitcast(I32), in_=w4_i[:, PASSES - 1, half:])
 
         tab_bytes = tab_plane[:].bitcast(U8)
         w4_bytes = w4_plane[:].bitcast(U8)
@@ -93,13 +100,16 @@ def tile_list_tablora_tm_none_kernel(tc, tab, w4_words, w4_scales, down, up, off
         def gather_scales(a):
             nc.vector.tensor_copy(v_scales[a][:], tab_bytes[:, a * T : (a + 1) * T].indirect(offsets[:]))
 
-        def group_down(a):
+        def shared_copy(dst, src, split):
+            if split > 0:
+                nc.vector.tensor_copy(out=dst[:, :split], in_=src[:, :split])
+            if split < dst.shape[1]:
+                nc.scalar.copy(out=dst[:, split:], in_=src[:, split:])
+
+        def group_down(a, split):
             src = d_raw[a][:].rearrange("p j (m t) -> p m j t", t=4)
             dst = d_grp[a][:].rearrange("p t m j -> p m j t")
-            if a < 2:
-                nc.scalar.copy(out=dst, in_=src)
-            else:
-                nc.vector.tensor_copy(out=dst, in_=src)
+            shared_copy(dst, src, split)
 
         def quantize_down(a):
             nc.vector.quantize_mx(
@@ -108,112 +118,106 @@ def tile_list_tablora_tm_none_kernel(tc, tab, w4_words, w4_scales, down, up, off
                 in_=d_grp[a][:].rearrange("p t m j -> p (t m j)"),
             )
 
-        def prepare_up(c):
-            n, first, width, v = U_STARTS[c] // N_TILE, U_STARTS[c] % N_TILE, U_WIDTHS[c], U_VECTOR[c]
-            src = u_raw[c][:].rearrange("p j (c i) -> p c j i", i=4)
-            dst = u_grp[n][:, first : first + width, :].rearrange("p (c i) j -> p c j i", i=4)
-            if v > 0:
-                nc.vector.tensor_copy(out=dst[:, 0 : v // 4], in_=src[:, 0 : v // 4])
-            if v < width:
-                nc.scalar.copy(out=dst[:, v // 4 : width // 4], in_=src[:, v // 4 : width // 4])
-            cols = slice(first, first + width)
+        def group_up(c, split):
+            raw = u_lo[:, :, CHUNK * c : CHUNK * (c + 1)] if c < 2 else u_hi[c - 2][:]
+            src = raw.rearrange("p j (c i) -> p c j i", i=4)
+            dst = u_grp[c][:].rearrange("p (c i) j -> p c j i", i=4)
+            shared_copy(dst, src, split // 4)
+
+        def quantize_up(c):
             nc.vector.quantize_mx(
-                out=u_codes[n][:, cols].bitcast(FP8X4),
-                scales=u_scales[n][:, cols],
-                in_=u_grp[n][:, cols, :].rearrange("p w j -> p (w j)"),
+                out=u_codes[c][:].bitcast(FP8X4), scales=u_scales[c][:], in_=u_grp[c][:].rearrange("p w j -> p (w j)")
             )
 
         def base(a, n):
+            if n == 0:
+                rhs = w4_lo[:, a, :]
+            else:
+                rhs = w4_hi[:, a, :] if a < PASSES - 1 else w4_last[:]
             for j in range(2):
                 js = slice(P * j, P * (j + 1))
                 nc.tensor.matmul_mx(
                     out=o_ps[j][n][:],
                     lhsT=v_codes[a][:, js].bitcast(FP8X4),
                     lhsT_scale=v_scales[a][:, js],
-                    rhs=w4[:, a, 1024 * n : 1024 * (n + 1)].bitcast(FP4X4),
+                    rhs=rhs.bitcast(FP4X4),
                     rhs_scale=w4_bytes[:, a * M + N_TILE * n : a * M + N_TILE * (n + 1)],
                     start=(a == 0),
                     stop=False,
                 )
 
         def low_rank(a):
-            for t in range(4):
-                ts = slice(P * t, P * (t + 1))
-                nc.tensor.matmul_mx(
-                    out=h_ps[t][:],
-                    lhsT=d_codes[a][:, ts].bitcast(FP8X4),
-                    lhsT_scale=d_scales[a][:, ts],
-                    rhs=v_codes[a][:].bitcast(FP8X4),
-                    rhs_scale=v_scales[a][:],
-                    start=(a == 0),
-                    stop=(a == PASSES - 1),
-                )
+            for j in range(2):
+                js = slice(P * j, P * (j + 1))
+                for t in range(4):
+                    ts = slice(P * t, P * (t + 1))
+                    nc.tensor.matmul_mx(
+                        out=h_ps[j][:, t, :],
+                        lhsT=d_codes[a][:, ts].bitcast(FP8X4),
+                        lhsT_scale=d_scales[a][:, ts],
+                        rhs=v_codes[a][:, js].bitcast(FP8X4),
+                        rhs_scale=v_scales[a][:, js],
+                        start=(a == 0 and t == 0),
+                        stop=(a == PASSES - 1 and t == 3),
+                    )
 
         def close(c):
-            n, first, width = U_STARTS[c] // N_TILE, U_STARTS[c] % N_TILE, U_WIDTHS[c]
-            cols = slice(first, first + width)
+            n, first = divmod(CHUNK * c, N_TILE)
             for j in range(2):
                 nc.tensor.matmul_mx(
-                    out=o_ps[j][n][:, cols],
-                    lhsT=h_codes[:, P * j : P * (j + 1)].bitcast(FP8X4),
-                    lhsT_scale=h_scales[:, P * j : P * (j + 1)],
-                    rhs=u_codes[n][:, cols].bitcast(FP8X4),
-                    rhs_scale=u_scales[n][:, cols],
+                    out=o_ps[j][n][:, first : first + CHUNK],
+                    lhsT=h_codes[j][:].bitcast(FP8X4),
+                    lhsT_scale=h_scales[j][:],
+                    rhs=u_codes[c][:].bitcast(FP8X4),
+                    rhs_scale=u_scales[c][:],
                     start=False,
-                    stop=(first + width == N_TILE),
+                    stop=(first + CHUNK == N_TILE),
                 )
 
-        def store(n, first, width):
-            cols = slice(first, first + width)
+        def store(n):
             for j in range(2):
-                if j == 0 and n == 1:
-                    nc.vector.tensor_copy(out=o_sb[j][n][:, cols], in_=o_ps[j][n][:, cols])
+                if j == 1 and n == 1:
+                    nc.vector.tensor_copy(out=o_sb[j][n][:], in_=o_ps[j][n][:])
                 else:
-                    nc.scalar.copy(out=o_sb[j][n][:, cols], in_=o_ps[j][n][:, cols])
-                nc.sync.dma_start(
-                    out=out[P * j : P * (j + 1), N_TILE * n + first : N_TILE * n + first + width],
-                    in_=o_sb[j][n][:, cols],
-                )
+                    nc.scalar.copy(out=o_sb[j][n][:], in_=o_ps[j][n][:])
+                nc.sync.dma_start(out=out[P * j : P * (j + 1), N_TILE * n : N_TILE * (n + 1)], in_=o_sb[j][n][:])
 
-        group_down(0)
+        group_down(0, 0)
         for a in range(PASSES):
             gather_scales(a)
-        group_down(1)
         quantize_down(0)
         gather_words(0)
         low_rank(0)
+        group_down(1, 0)
+        group_down(2, D_SPLIT)
         quantize_down(1)
         gather_words(1)
-        low_rank(1)
-        group_down(2)
         quantize_down(2)
-        for a in range(2):
-            for n in range(2):
-                base(a, n)
+        low_rank(1)
         gather_words(2)
         low_rank(2)
-        base(2, 0)
-        base(2, 1)
-        for t in range(4):
-            if t < 2:
-                nc.vector.tensor_copy(out=h_raw[:, t, :], in_=h_ps[t][:])
-            else:
-                nc.scalar.copy(out=h_raw[:, t, :], in_=h_ps[t][:])
-        nc.vector.tensor_copy(
-            out=h_grp[:].rearrange("p (c i) t -> p c t i", i=8),
-            in_=h_raw[:].rearrange("p t (c i) -> p c t i", i=8),
-        )
-        nc.vector.quantize_mx(
-            out=h_codes[:].bitcast(FP8X4), scales=h_scales[:], in_=h_grp[:].rearrange("p w j -> p (w j)")
-        )
-        prepare_up(0)
-        prepare_up(1)
+        for a in range(PASSES):
+            base(a, 0)
+        nc.scalar.copy(out=h_grp[0][:], in_=h_ps[0][:].rearrange("p t n -> p n t"))
+        nc.vector.tensor_copy(out=h_grp[1][:], in_=h_ps[1][:].rearrange("p t n -> p n t"))
+        for j in range(2):
+            nc.vector.quantize_mx(
+                out=h_codes[j][:].bitcast(FP8X4), scales=h_scales[j][:], in_=h_grp[j][:].rearrange("p w j -> p (w j)")
+            )
+        group_up(0, CHUNK)
+        group_up(1, 0)
+        base(0, 1)
+        base(1, 1)
+        quantize_up(0)
+        quantize_up(1)
         close(0)
         close(1)
-        prepare_up(2)
-        store(0, 0, N_TILE)
+        group_up(2, CHUNK)
+        store(0)
+        quantize_up(2)
         close(2)
-        prepare_up(3)
+        group_up(3, U_SPLIT)
+        base(2, 1)
+        quantize_up(3)
         close(3)
-        store(1, 0, N_TILE // 2)
-        store(1, N_TILE // 2, N_TILE // 2)
+        store(1)

@@ -18,6 +18,7 @@ P = 128
 PASSES = K // 512
 N_TILE = 512
 CHUNK = 256
+GROUPS = ((0, 512), (512, 256), (768, 256))
 WORD_COLS = 512 * T // 4
 D_SPLIT = 88
 U_SPLIT = 176
@@ -33,15 +34,16 @@ def tile_list_tablora_tm_none_kernel(tc, tab, w4_words, w4_scales, down, up, off
         words = [keep.tile([P, T], I32, name=f"words{a}", align_bytes=64) for a in range(PASSES)]
         tab_plane = keep.tile([P, PASSES * T // 4], I32, name="tab_plane", align_bytes=64)
         w4_plane = keep.tile([P, PASSES * M // 4], I32, name="w4_plane", align_bytes=64)
-        w4_lo = keep.tile([P, PASSES, 2 * N_TILE], U8, name="w4_lo", align_bytes=64)
-        w4_hi = keep.tile([P, PASSES - 1, 2 * N_TILE], U8, name="w4_hi", align_bytes=64)
-        w4_last = keep.tile([P, 2 * N_TILE], U8, name="w4_last", align_bytes=64)
+        w4_first = keep.tile([P, 2 * M], U8, name="w4_first", align_bytes=64)
+        w4_rest = [
+            keep.tile([P, PASSES - 1, 2 * width], U8, name=f"w4_rest{g}", align_bytes=64)
+            for g, (first, width) in enumerate(GROUPS)
+        ]
         d_raw = [keep.tile([P, 4, R], F32, name=f"d_raw{a}", align_bytes=64) for a in range(PASSES)]
         d_grp = [keep.tile([P, 4, P, 4], BF16, name=f"d_grp{a}", align_bytes=64) for a in range(PASSES)]
         d_codes = [keep.tile([P, R], U32, name=f"d_codes{a}", align_bytes=64) for a in range(PASSES)]
         d_scales = [keep.tile([P, R], U8, name=f"d_scales{a}", align_bytes=64) for a in range(PASSES)]
-        u_lo = keep.tile([P, 4, N_TILE], F32, name="u_lo", align_bytes=64)
-        u_hi = [keep.tile([P, 4, CHUNK], F32, name=f"u_hi{c}", align_bytes=64) for c in range(2)]
+        u_raw = [keep.tile([P, 4, CHUNK], F32, name=f"u_raw{c}", align_bytes=64) for c in range(4)]
         u_grp = [keep.tile([P, CHUNK, 4], BF16, name=f"u_grp{c}", align_bytes=64) for c in range(4)]
         u_codes = [keep.tile([P, CHUNK], U32, name=f"u_codes{c}", align_bytes=64) for c in range(4)]
         u_scales = [keep.tile([P, CHUNK], U8, name=f"u_scales{c}", align_bytes=64) for c in range(4)]
@@ -50,9 +52,14 @@ def tile_list_tablora_tm_none_kernel(tc, tab, w4_words, w4_scales, down, up, off
         h_grp = [keep.tile([P, P, 4], BF16, name=f"h_grp{j}", align_bytes=64) for j in range(2)]
         h_codes = [keep.tile([P, P], U32, name=f"h_codes{j}", align_bytes=64) for j in range(2)]
         h_scales = [keep.tile([P, P], U8, name=f"h_scales{j}", align_bytes=64) for j in range(2)]
-        o_sb = [[keep.tile([P, N_TILE], F32, name=f"o_sb{j}{n}", align_bytes=64) for n in range(2)] for j in range(2)]
+        o_sb = [
+            [keep.tile([P, width], F32, name=f"o_sb{j}{g}", align_bytes=64) for g, (first, width) in enumerate(GROUPS)]
+            for j in range(2)
+        ]
         h_ps = [psum.tile([P, 4, P], F32, name=f"h_ps{j}") for j in range(2)]
-        o_ps = [[psum.tile([P, N_TILE], F32, name=f"o_ps{j}{n}") for n in range(2)] for j in range(2)]
+        o_ps = [
+            [psum.tile([P, width], F32, name=f"o_ps{j}{g}") for g, (first, width) in enumerate(GROUPS)] for j in range(2)
+        ]
 
         nc.vector.memset(tab_plane[:], 0)
         nc.vector.memset(w4_plane[:], 0)
@@ -62,7 +69,6 @@ def tile_list_tablora_tm_none_kernel(tc, tab, w4_words, w4_scales, down, up, off
         w4_s = w4_scales.bitcast(I32).rearrange("a (q r) n -> r q a n", q=4, r=4)
         w4_i = w4_words.bitcast(I32).rearrange("a p n -> p a n")
         up_v = up.rearrange("(p j) n -> p j n", j=4)
-        half = N_TILE // 2
 
         def load_words(a):
             nc.sync.dma_start(out=words[a][:], in_=tab_i[a, :WORD_COLS].rearrange("(p t) -> p t", p=P))
@@ -76,20 +82,28 @@ def tile_list_tablora_tm_none_kernel(tc, tab, w4_words, w4_scales, down, up, off
             for r in range(4):
                 nc.sync.dma_start(out=plane[r:P:32, :].rearrange("q (a t) -> q a t", a=PASSES), in_=rows[r])
 
+        def load_w4(g):
+            first, width = GROUPS[g]
+            nc.sync.dma_start(out=w4_rest[g][:].bitcast(I32), in_=w4_i[:, 1:, first // 2 : (first + width) // 2])
+
+        def load_up(c):
+            nc.sync.dma_start(out=u_raw[c][:], in_=up_v[:, :, CHUNK * c : CHUNK * (c + 1)])
+
         load_down(0)
         load_scales(tab_plane, tab_s)
-        load_scales(w4_plane, w4_s)
-        load_words(0)
         load_down(1)
-        load_down(2)
+        load_words(0)
         load_words(1)
+        load_down(2)
         load_words(2)
-        nc.sync.dma_start(out=w4_lo[:].bitcast(I32), in_=w4_i[:, :, :half])
-        nc.sync.dma_start(out=u_lo[:], in_=up_v[:, :, :N_TILE])
-        nc.sync.dma_start(out=w4_hi[:].bitcast(I32), in_=w4_i[:, : PASSES - 1, half:])
-        for c in range(2):
-            nc.sync.dma_start(out=u_hi[c][:], in_=up_v[:, :, N_TILE + CHUNK * c : N_TILE + CHUNK * (c + 1)])
-        nc.sync.dma_start(out=w4_last[:].bitcast(I32), in_=w4_i[:, PASSES - 1, half:])
+        load_scales(w4_plane, w4_s)
+        nc.sync.dma_start(out=w4_first[:].bitcast(I32), in_=w4_i[:, 0, :])
+        load_w4(0)
+        for c in range(3):
+            load_up(c)
+        load_w4(1)
+        load_up(3)
+        load_w4(2)
 
         tab_bytes = tab_plane[:].bitcast(U8)
         w4_bytes = w4_plane[:].bitcast(U8)
@@ -119,8 +133,7 @@ def tile_list_tablora_tm_none_kernel(tc, tab, w4_words, w4_scales, down, up, off
             )
 
         def group_up(c, split):
-            raw = u_lo[:, :, CHUNK * c : CHUNK * (c + 1)] if c < 2 else u_hi[c - 2][:]
-            src = raw.rearrange("p j (c i) -> p c j i", i=4)
+            src = u_raw[c][:].rearrange("p j (c i) -> p c j i", i=4)
             dst = u_grp[c][:].rearrange("p (c i) j -> p c j i", i=4)
             shared_copy(dst, src, split // 4)
 
@@ -129,22 +142,25 @@ def tile_list_tablora_tm_none_kernel(tc, tab, w4_words, w4_scales, down, up, off
                 out=u_codes[c][:].bitcast(FP8X4), scales=u_scales[c][:], in_=u_grp[c][:].rearrange("p w j -> p (w j)")
             )
 
-        def base(a, n):
-            if n == 0:
-                rhs = w4_lo[:, a, :]
-            else:
-                rhs = w4_hi[:, a, :] if a < PASSES - 1 else w4_last[:]
+        def base(a, g):
+            first, width = GROUPS[g]
+            step = N_TILE if width == N_TILE else P
             for j in range(2):
                 js = slice(P * j, P * (j + 1))
-                nc.tensor.matmul_mx(
-                    out=o_ps[j][n][:],
-                    lhsT=v_codes[a][:, js].bitcast(FP8X4),
-                    lhsT_scale=v_scales[a][:, js],
-                    rhs=rhs.bitcast(FP4X4),
-                    rhs_scale=w4_bytes[:, a * M + N_TILE * n : a * M + N_TILE * (n + 1)],
-                    start=(a == 0),
-                    stop=False,
-                )
+                for c in range(0, width, step):
+                    if a == 0:
+                        rhs = w4_first[:, 2 * (first + c) : 2 * (first + c + step)]
+                    else:
+                        rhs = w4_rest[g][:, a - 1, 2 * c : 2 * (c + step)]
+                    nc.tensor.matmul_mx(
+                        out=o_ps[j][g][:, c : c + step],
+                        lhsT=v_codes[a][:, js].bitcast(FP8X4),
+                        lhsT_scale=v_scales[a][:, js],
+                        rhs=rhs.bitcast(FP4X4),
+                        rhs_scale=w4_bytes[:, a * M + first + c : a * M + first + c + step],
+                        start=(a == 0 and c == 0),
+                        stop=False,
+                    )
 
         def low_rank(a):
             for j in range(2):
@@ -161,26 +177,40 @@ def tile_list_tablora_tm_none_kernel(tc, tab, w4_words, w4_scales, down, up, off
                         stop=(a == PASSES - 1 and t == 3),
                     )
 
+        def group_h(j, on_vector):
+            src = h_ps[j][:].rearrange("p t n -> p n t")
+            if on_vector:
+                nc.vector.tensor_copy(out=h_grp[j][:], in_=src)
+            else:
+                nc.scalar.copy(out=h_grp[j][:], in_=src)
+
+        def quantize_h(j):
+            nc.vector.quantize_mx(
+                out=h_codes[j][:].bitcast(FP8X4), scales=h_scales[j][:], in_=h_grp[j][:].rearrange("p w j -> p (w j)")
+            )
+
         def close(c):
-            n, first = divmod(CHUNK * c, N_TILE)
+            g = max(c - 1, 0)
+            first = CHUNK * c - GROUPS[g][0]
             for j in range(2):
                 nc.tensor.matmul_mx(
-                    out=o_ps[j][n][:, first : first + CHUNK],
+                    out=o_ps[j][g][:, first : first + CHUNK],
                     lhsT=h_codes[j][:].bitcast(FP8X4),
                     lhsT_scale=h_scales[j][:],
                     rhs=u_codes[c][:].bitcast(FP8X4),
                     rhs_scale=u_scales[c][:],
                     start=False,
-                    stop=(first + CHUNK == N_TILE),
+                    stop=(first + CHUNK == GROUPS[g][1]),
                 )
 
-        def store(n):
+        def store(g, on_vector):
+            first, width = GROUPS[g]
             for j in range(2):
-                if j == 1 and n == 1:
-                    nc.vector.tensor_copy(out=o_sb[j][n][:], in_=o_ps[j][n][:])
+                if j in on_vector:
+                    nc.vector.tensor_copy(out=o_sb[j][g][:], in_=o_ps[j][g][:])
                 else:
-                    nc.scalar.copy(out=o_sb[j][n][:], in_=o_ps[j][n][:])
-                nc.sync.dma_start(out=out[P * j : P * (j + 1), N_TILE * n : N_TILE * (n + 1)], in_=o_sb[j][n][:])
+                    nc.scalar.copy(out=o_sb[j][g][:], in_=o_ps[j][g][:])
+                nc.sync.dma_start(out=out[P * j : P * (j + 1), first : first + width], in_=o_sb[j][g][:])
 
         group_down(0, 0)
         for a in range(PASSES):
@@ -189,35 +219,34 @@ def tile_list_tablora_tm_none_kernel(tc, tab, w4_words, w4_scales, down, up, off
         gather_words(0)
         low_rank(0)
         group_down(1, 0)
-        group_down(2, D_SPLIT)
-        quantize_down(1)
         gather_words(1)
-        quantize_down(2)
+        quantize_down(1)
         low_rank(1)
+        group_down(2, D_SPLIT)
+        quantize_down(2)
         gather_words(2)
         low_rank(2)
+        group_h(0, False)
+        group_h(1, True)
+        quantize_h(0)
+        quantize_h(1)
         for a in range(PASSES):
             base(a, 0)
-        nc.scalar.copy(out=h_grp[0][:], in_=h_ps[0][:].rearrange("p t n -> p n t"))
-        nc.vector.tensor_copy(out=h_grp[1][:], in_=h_ps[1][:].rearrange("p t n -> p n t"))
-        for j in range(2):
-            nc.vector.quantize_mx(
-                out=h_codes[j][:].bitcast(FP8X4), scales=h_scales[j][:], in_=h_grp[j][:].rearrange("p w j -> p (w j)")
-            )
-        group_up(0, CHUNK)
-        group_up(1, 0)
         base(0, 1)
-        base(1, 1)
-        quantize_up(0)
-        quantize_up(1)
+        base(0, 2)
+        for c in range(3):
+            group_up(c, U_SPLIT)
+            quantize_up(c)
         close(0)
         close(1)
-        group_up(2, CHUNK)
-        store(0)
-        quantize_up(2)
-        close(2)
-        group_up(3, U_SPLIT)
+        store(0, ())
+        base(1, 1)
         base(2, 1)
+        close(2)
+        group_up(3, CHUNK)
+        store(1, ())
+        base(1, 2)
+        base(2, 2)
         quantize_up(3)
         close(3)
-        store(1)
+        store(2, (1,))

@@ -121,9 +121,11 @@ def tile_list_tablora_tm_none_kernel(tc, tab, w4_words, w4_scales, down, up, off
                 nc.scalar.copy(out=dst[:, split:], in_=src[:, split:])
 
         def group_down(a, split):
-            src = d_raw[a][:].rearrange("p j (m t) -> p m j t", t=4)
-            dst = d_grp[a][:].rearrange("p t m j -> p m j t")
-            shared_copy(dst, src, split)
+            src = d_raw[a][:].rearrange("p j (m u e) -> p u m j e", u=2, e=2)
+            dst = d_grp[a][:].rearrange("p (u e) m j -> p u m j e", e=2)
+            if split > 0:
+                nc.vector.tensor_copy(out=dst[:, :, :split], in_=src[:, :, :split])
+            nc.scalar.copy(out=dst[:, :, split:], in_=src[:, :, split:])
 
         def quantize_down(a):
             nc.vector.quantize_mx(

@@ -32,7 +32,9 @@ def tile_list_tablora_tm_none_kernel(tc, tab, w4_words, w4_scales, down, up, off
 
         offsets = keep.tile([P, S // 16], U16, name="offsets")
         words = [keep.tile([P, T], I32, name=f"words{a}", align_bytes=64) for a in range(PASSES)]
-        tab_plane = keep.tile([P, PASSES * T // 4], I32, name="tab_plane", align_bytes=64)
+        tab_rows = keep.tile([P, T // 4], I32, name="tab_rows", align_bytes=64)
+        picked_rows = keep.tile([P, S], U8, name="picked_rows", align_bytes=64)
+        v_plane = keep.tile([P, PASSES * S // 4], I32, name="v_plane", align_bytes=64)
         w4_plane = keep.tile([P, PASSES * M // 4], I32, name="w4_plane", align_bytes=64)
         w4_first = keep.tile([P, 2 * M], U8, name="w4_first", align_bytes=64)
         w4_rest = [
@@ -43,12 +45,13 @@ def tile_list_tablora_tm_none_kernel(tc, tab, w4_words, w4_scales, down, up, off
         d_grp = [keep.tile([P, 4, P, 4], BF16, name=f"d_grp{a}", align_bytes=64) for a in range(PASSES)]
         d_codes = [keep.tile([P, R], U32, name=f"d_codes{a}", align_bytes=64) for a in range(PASSES)]
         d_scales = [keep.tile([P, R], U8, name=f"d_scales{a}", align_bytes=64) for a in range(PASSES)]
-        u_raw = [keep.tile([P, 4, CHUNK], F32, name=f"u_raw{c}", align_bytes=64) for c in range(4)]
+        u_raw = [
+            keep.tile([P, 4, width], F32, name=f"u_raw{g}", align_bytes=64) for g, (first, width) in enumerate(GROUPS)
+        ]
         u_grp = [keep.tile([P, CHUNK, 4], BF16, name=f"u_grp{c}", align_bytes=64) for c in range(4)]
         u_codes = [keep.tile([P, CHUNK], U32, name=f"u_codes{c}", align_bytes=64) for c in range(4)]
         u_scales = [keep.tile([P, CHUNK], U8, name=f"u_scales{c}", align_bytes=64) for c in range(4)]
         v_codes = [keep.tile([P, S], U32, name=f"v_codes{a}", align_bytes=64) for a in range(PASSES)]
-        v_scales = [keep.tile([P, S], U8, name=f"v_scales{a}", align_bytes=64) for a in range(PASSES)]
         h_grp = [keep.tile([P, P, 4], BF16, name=f"h_grp{j}", align_bytes=64) for j in range(2)]
         h_codes = [keep.tile([P, P], U32, name=f"h_codes{j}", align_bytes=64) for j in range(2)]
         h_scales = [keep.tile([P, P], U8, name=f"h_scales{j}", align_bytes=64) for j in range(2)]
@@ -61,11 +64,12 @@ def tile_list_tablora_tm_none_kernel(tc, tab, w4_words, w4_scales, down, up, off
             [psum.tile([P, width], F32, name=f"o_ps{j}{g}") for g, (first, width) in enumerate(GROUPS)] for j in range(2)
         ]
 
-        nc.vector.memset(tab_plane[:], 0)
+        nc.vector.memset(tab_rows[:], 0)
+        nc.vector.memset(v_plane[:], 0)
         nc.vector.memset(w4_plane[:], 0)
         nc.sync.dma_start(offsets[:], offs)
         tab_i = tab.bitcast(I32)
-        tab_s = tab_i[:, WORD_COLS:].rearrange("a (q r t) -> r q a t", q=4, r=4)
+        tab_s = tab_i[:, WORD_COLS:].rearrange("a (q t) -> q a t", q=16)
         w4_s = w4_scales.bitcast(I32).rearrange("a (q r) n -> r q a n", q=4, r=4)
         w4_i = w4_words.bitcast(I32).rearrange("a p n -> p a n")
         up_v = up.rearrange("(p j) n -> p j n", j=4)
@@ -86,33 +90,33 @@ def tile_list_tablora_tm_none_kernel(tc, tab, w4_words, w4_scales, down, up, off
             first, width = GROUPS[g]
             nc.sync.dma_start(out=w4_rest[g][:].bitcast(I32), in_=w4_i[:, 1:, first // 2 : (first + width) // 2])
 
-        def load_up(c):
-            nc.sync.dma_start(out=u_raw[c][:], in_=up_v[:, :, CHUNK * c : CHUNK * (c + 1)])
+        def load_up(g):
+            first, width = GROUPS[g]
+            nc.sync.dma_start(out=u_raw[g][:], in_=up_v[:, :, first : first + width])
 
         load_down(0)
-        load_scales(tab_plane, tab_s)
+        nc.sync.dma_start(out=tab_rows[0 : 2 * 16 * PASSES : 2, :], in_=tab_s)
+        nc.vector.tensor_copy(picked_rows[:], tab_rows[:].bitcast(U8).indirect(offsets[:]))
         load_down(1)
         load_words(0)
         load_words(1)
         load_down(2)
+        for q in range(4):
+            nc.sync.dma_start(
+                out=v_plane[32 * q : 32 * q + 4, :], in_=picked_rows[24 * q : 24 * (q + 1) : 2, :].bitcast(I32)
+            )
         load_words(2)
         load_scales(w4_plane, w4_s)
         nc.sync.dma_start(out=w4_first[:].bitcast(I32), in_=w4_i[:, 0, :])
-        load_w4(0)
-        for c in range(3):
-            load_up(c)
-        load_w4(1)
-        load_up(3)
-        load_w4(2)
+        for g in range(3):
+            load_up(g)
+            load_w4(g)
 
-        tab_bytes = tab_plane[:].bitcast(U8)
+        v_scales = [v_plane[:].bitcast(U8)[:, S * a : S * (a + 1)] for a in range(PASSES)]
         w4_bytes = w4_plane[:].bitcast(U8)
 
         def gather_words(a):
             nc.vector.tensor_copy(v_codes[a][:], words[a][:].bitcast(U32).indirect(offsets[:]))
-
-        def gather_scales(a):
-            nc.vector.tensor_copy(v_scales[a][:], tab_bytes[:, a * T : (a + 1) * T].indirect(offsets[:]))
 
         def shared_copy(dst, src, split):
             if split > 0:
@@ -135,7 +139,9 @@ def tile_list_tablora_tm_none_kernel(tc, tab, w4_words, w4_scales, down, up, off
             )
 
         def group_up(c, split):
-            src = u_raw[c][:].rearrange("p j (c i) -> p c j i", i=4)
+            g = max(c - 1, 0)
+            first = CHUNK * c - GROUPS[g][0]
+            src = u_raw[g][:, :, first : first + CHUNK].rearrange("p j (c i) -> p c j i", i=4)
             dst = u_grp[c][:].rearrange("p (c i) j -> p c j i", i=4)
             shared_copy(dst, src, split // 4)
 
@@ -215,8 +221,6 @@ def tile_list_tablora_tm_none_kernel(tc, tab, w4_words, w4_scales, down, up, off
                 nc.sync.dma_start(out=out[P * j : P * (j + 1), first : first + width], in_=o_sb[j][g][:])
 
         group_down(0, 0)
-        for a in range(PASSES):
-            gather_scales(a)
         quantize_down(0)
         gather_words(0)
         low_rank(0)
@@ -232,18 +236,20 @@ def tile_list_tablora_tm_none_kernel(tc, tab, w4_words, w4_scales, down, up, off
         group_h(1, True)
         quantize_h(0)
         quantize_h(1)
-        for a in range(PASSES):
-            base(a, 0)
-        base(0, 1)
-        base(0, 2)
-        for c in range(3):
-            group_up(c, U_SPLIT)
+        for g in range(3):
+            base(0, g)
+        group_up(0, U_SPLIT)
+        group_up(1, U_SPLIT)
+        base(1, 0)
+        base(2, 0)
+        for c in range(2):
             quantize_up(c)
-        close(0)
-        close(1)
+            close(c)
+        group_up(2, U_SPLIT)
         store(0, ())
         base(1, 1)
         base(2, 1)
+        quantize_up(2)
         close(2)
         group_up(3, CHUNK)
         store(1, ())

@@ -16,12 +16,19 @@ FP4X4 = mybir.dt.float4_e2m1fn_x4
 
 P = 128
 PASSES = K // 512
-N_TILE = 512
-CHUNK = 256
-GROUPS = ((0, 512), (512, 256), (768, 256))
+GROUPS = ((0, 512), (512, 256), (768, 128), (896, 128))
+CHUNKS = ((0, 0, 256), (0, 256, 256), (1, 0, 256), (2, 0, 128), (3, 0, 128))
+UP_LOADS = ((0, 512), (512, 256), (768, 128), (896, 128))
+W4_LOADS = ((0, 3, 0, 512), (0, 3, 512, 384), (0, 3, 896, 128))
+WORD_LOADS = ((0, 2), (2, 1))
+SPLIT_BANKS = (0, 3)
+LOADS = (('down', 0), ('list',), ('ts', 'sync'), ('ws', 'sync'), ('gs',), ('down', 1), ('words', 0), ('down', 2), ('mv', 'sync'), ('words', 1), ('w4', 0), ('up', 0), ('w4', 1), ('up', 1), ('up', 2), ('up', 3), ('w4', 2))
+STEPS = (('gd', 0, 0), ('qd', 0), ('gw', 0), ('lr', 0), ('gd', 1, 0), ('gw', 1), ('qd', 1), ('lr', 1), ('gd', 2, 88), ('qd', 2), ('gw', 2), ('lr', 2), ('gh', 0, 0), ('gh', 1, 1), ('qh', 0), ('qh', 1), ('base', 0, 0), ('base', 1, 0), ('base', 2, 0), ('gu', 0, 176), ('gu', 1, 176), ('qu', 0), ('close', 0), ('qu', 1), ('close', 1), ('base', 0, 1), ('base', 1, 1), ('base', 2, 1), ('base', 0, 2), ('base', 1, 2), ('base', 2, 2), ('gu', 2, 176), ('store', 0, (), 1), ('qu', 2), ('close', 2), ('gu', 3, 128), ('qu', 3), ('store', 1, (), 0), ('close', 3), ('gu', 4, 128), ('base', 0, 3), ('base', 1, 3), ('base', 2, 3), ('qu', 4), ('store', 2, (), 0), ('close', 4), ('store', 3, (1,), 0))
+MERGED = True
 WORD_COLS = 512 * T // 4
-D_SPLIT = 88
-U_SPLIT = 176
+W4_COLS = PASSES * M // 4
+ROW0, STEP = 32, 4
+V_COLS = PASSES * S // 4
 
 
 def tile_list_tablora_tm_none_kernel(tc, tab, w4_words, w4_scales, down, up, offs, out):
@@ -31,105 +38,124 @@ def tile_list_tablora_tm_none_kernel(tc, tab, w4_words, w4_scales, down, up, off
         psum = ctx.enter_context(tc.psum_pool(name="psum", bufs=1))
 
         offsets = keep.tile([P, S // 16], U16, name="offsets")
-        words = [keep.tile([P, T], I32, name=f"words{a}", align_bytes=64) for a in range(PASSES)]
-        tab_rows = keep.tile([P, T // 4], I32, name="tab_rows", align_bytes=64)
-        picked_rows = keep.tile([P, S], U8, name="picked_rows", align_bytes=64)
-        v_plane = keep.tile([P, PASSES * S // 4], I32, name="v_plane", align_bytes=64)
-        w4_plane = keep.tile([P, PASSES * M // 4], I32, name="w4_plane", align_bytes=64)
-        w4_first = keep.tile([P, 2 * M], U8, name="w4_first", align_bytes=64)
-        w4_rest = [
-            keep.tile([P, PASSES - 1, 2 * width], U8, name=f"w4_rest{g}", align_bytes=64)
-            for g, (first, width) in enumerate(GROUPS)
+        words = [keep.tile([P, n, T], I32, name=f"words{a}", align_bytes=64) for a, n in WORD_LOADS]
+        tab_rows = keep.tile([P, PASSES * T // 4], I32, name="tab_rows", align_bytes=64)
+        picked_rows = keep.tile([P, PASSES * S], U8, name="picked_rows", align_bytes=64)
+        if MERGED:
+            stage = keep.tile([P, W4_COLS + V_COLS], I32, name="stage", align_bytes=64)
+            plane = keep.tile([P, W4_COLS + V_COLS], I32, name="plane", align_bytes=64)
+            w4_plane = plane[:, :W4_COLS]
+            v_plane = plane[:, W4_COLS:]
+        else:
+            w4_plane = keep.tile([P, W4_COLS], I32, name="w4_plane", align_bytes=64)[:]
+            v_plane = keep.tile([P, V_COLS], I32, name="v_plane", align_bytes=64)[:]
+        w4_sb = [
+            keep.tile([P, n, 2 * width], U8, name=f"w4_sb{i}", align_bytes=64)
+            for i, (a, n, first, width) in enumerate(W4_LOADS)
         ]
         d_raw = [keep.tile([P, 4, R], F32, name=f"d_raw{a}", align_bytes=64) for a in range(PASSES)]
         d_grp = [keep.tile([P, 4, P, 4], BF16, name=f"d_grp{a}", align_bytes=64) for a in range(PASSES)]
         d_codes = [keep.tile([P, R], U32, name=f"d_codes{a}", align_bytes=64) for a in range(PASSES)]
         d_scales = [keep.tile([P, R], U8, name=f"d_scales{a}", align_bytes=64) for a in range(PASSES)]
         u_raw = [
-            keep.tile([P, 4, width], F32, name=f"u_raw{g}", align_bytes=64) for g, (first, width) in enumerate(GROUPS)
+            keep.tile([P, 4, width], F32, name=f"u_raw{g}", align_bytes=64) for g, (first, width) in enumerate(UP_LOADS)
         ]
-        u_grp = [keep.tile([P, CHUNK, 4], BF16, name=f"u_grp{c}", align_bytes=64) for c in range(4)]
-        u_codes = [keep.tile([P, CHUNK], U32, name=f"u_codes{c}", align_bytes=64) for c in range(4)]
-        u_scales = [keep.tile([P, CHUNK], U8, name=f"u_scales{c}", align_bytes=64) for c in range(4)]
+        u_grp = [keep.tile([P, w, 4], BF16, name=f"u_grp{c}", align_bytes=64) for c, (g, f, w) in enumerate(CHUNKS)]
+        u_codes = [keep.tile([P, w], U32, name=f"u_codes{c}", align_bytes=64) for c, (g, f, w) in enumerate(CHUNKS)]
+        u_scales = [keep.tile([P, w], U8, name=f"u_scales{c}", align_bytes=64) for c, (g, f, w) in enumerate(CHUNKS)]
         v_codes = [keep.tile([P, S], U32, name=f"v_codes{a}", align_bytes=64) for a in range(PASSES)]
         h_grp = [keep.tile([P, P, 4], BF16, name=f"h_grp{j}", align_bytes=64) for j in range(2)]
         h_codes = [keep.tile([P, P], U32, name=f"h_codes{j}", align_bytes=64) for j in range(2)]
         h_scales = [keep.tile([P, P], U8, name=f"h_scales{j}", align_bytes=64) for j in range(2)]
         o_sb = [
-            [keep.tile([P, width], F32, name=f"o_sb{j}{g}", align_bytes=64) for g, (first, width) in enumerate(GROUPS)]
-            for j in range(2)
+            keep.tile([P, 2, width], F32, name=f"o_sb{g}", align_bytes=64) for g, (first, width) in enumerate(GROUPS)
         ]
         h_ps = [psum.tile([P, 4, P], F32, name=f"h_ps{j}") for j in range(2)]
-        o_ps = [
-            [psum.tile([P, width], F32, name=f"o_ps{j}{g}") for g, (first, width) in enumerate(GROUPS)] for j in range(2)
-        ]
+        o_ps = []
+        for g, (first, width) in enumerate(GROUPS):
+            if g in SPLIT_BANKS:
+                o_ps.append([psum.tile([P, width], F32, name=f"o_ps{g}{j}")[:] for j in range(2)])
+            else:
+                both = psum.tile([P, 2, width], F32, name=f"o_ps{g}")
+                o_ps.append([both[:, 0, :], both[:, 1, :], both[:]])
 
         nc.vector.memset(tab_rows[:], 0)
-        nc.vector.memset(v_plane[:], 0)
-        nc.vector.memset(w4_plane[:], 0)
-        nc.sync.dma_start(offsets[:], offs)
+        if MERGED:
+            nc.vector.memset(plane[:], 0)
+        else:
+            nc.vector.memset(v_plane, 0)
+            nc.vector.memset(w4_plane, 0)
         tab_i = tab.bitcast(I32)
         tab_s = tab_i[:, WORD_COLS:].rearrange("a (q t) -> q a t", q=16)
-        w4_s = w4_scales.bitcast(I32).rearrange("a (q r) n -> r q a n", q=4, r=4)
         w4_i = w4_words.bitcast(I32).rearrange("a p n -> p a n")
         up_v = up.rearrange("(p j) n -> p j n", j=4)
+        out_v = out.rearrange("(j p) n -> p j n", j=2)
+        queues = {"sync": nc.sync, "scalar": nc.scalar, "gpsimd": nc.gpsimd}
 
-        def load_words(a):
-            nc.sync.dma_start(out=words[a][:], in_=tab_i[a, :WORD_COLS].rearrange("(p t) -> p t", p=P))
+        def load_list():
+            nc.sync.dma_start(offsets[:], offs)
 
         def load_down(a):
             nc.sync.dma_start(
                 out=d_raw[a][:], in_=down[512 * a : 512 * (a + 1), :].rearrange("(p j) r -> p j r", j=4)
             )
 
-        def load_scales(plane, rows):
+        def load_words(i):
+            a, n = WORD_LOADS[i]
+            nc.sync.dma_start(out=words[i][:], in_=tab_i[a : a + n, :WORD_COLS].rearrange("a (p t) -> p a t", p=P))
+
+        def load_w4(i):
+            a, n, first, width = W4_LOADS[i]
+            nc.sync.dma_start(out=w4_sb[i][:].bitcast(I32), in_=w4_i[:, a : a + n, first // 2 : (first + width) // 2])
+
+        def load_up(i):
+            first, width = UP_LOADS[i]
+            nc.sync.dma_start(out=u_raw[i][:], in_=up_v[:, :, first : first + width])
+
+        def load_tab_scales(queue):
+            queues[queue].dma_start(out=tab_rows[ROW0 : ROW0 + 16 * STEP - STEP + 1 : STEP, :].rearrange("q (a t) -> q a t", a=PASSES), in_=tab_s)
+
+        def gather_scales():
+            tab_bytes = tab_rows[:].bitcast(U8)
+            for a in range(PASSES):
+                nc.vector.tensor_copy(
+                    picked_rows[:, S * a : S * (a + 1)], tab_bytes[:, T * a : T * (a + 1)].indirect(offsets[:])
+                )
+            if MERGED:
+                nc.vector.tensor_copy(out=stage[:, W4_COLS:], in_=picked_rows[:].bitcast(I32))
+
+        def load_w4_scales(queue):
+            if MERGED:
+                w4_s = w4_scales.bitcast(I32).rearrange("a q n -> q a n")
+                queues[queue].dma_start(out=stage[ROW0 : ROW0 + 16 * STEP - STEP + 1 : STEP, :W4_COLS].rearrange("q (a n) -> q a n", a=PASSES), in_=w4_s)
+            else:
+                w4_s = w4_scales.bitcast(I32).rearrange("a (q r) n -> r q a n", q=4, r=4)
+                for r in range(4):
+                    queues[queue].dma_start(
+                        out=w4_plane[r:P:32, :].rearrange("q (a t) -> q a t", a=PASSES), in_=w4_s[r]
+                    )
+
+        def move_scales(queue):
             for r in range(4):
-                nc.sync.dma_start(out=plane[r:P:32, :].rearrange("q (a t) -> q a t", a=PASSES), in_=rows[r])
+                if MERGED:
+                    queues[queue].dma_start(out=plane[r:P:32, :], in_=stage[ROW0 + STEP * r : ROW0 + STEP * (r + 12) + 1 : 4 * STEP, :])
+                else:
+                    queues[queue].dma_start(out=v_plane[r:P:32, :], in_=picked_rows[ROW0 + STEP * r : ROW0 + STEP * (r + 12) + 1 : 4 * STEP, :].bitcast(I32))
 
-        def load_w4(g):
-            first, width = GROUPS[g]
-            nc.sync.dma_start(out=w4_rest[g][:].bitcast(I32), in_=w4_i[:, 1:, first // 2 : (first + width) // 2])
-
-        def load_up(g):
-            first, width = GROUPS[g]
-            nc.sync.dma_start(out=u_raw[g][:], in_=up_v[:, :, first : first + width])
-
-        load_down(0)
-        nc.sync.dma_start(out=tab_rows[0 : 2 * 16 * PASSES : 2, :], in_=tab_s)
-        nc.vector.tensor_copy(picked_rows[:], tab_rows[:].bitcast(U8).indirect(offsets[:]))
-        load_down(1)
-        load_words(0)
-        load_words(1)
-        load_down(2)
-        for q in range(4):
-            nc.sync.dma_start(
-                out=v_plane[32 * q : 32 * q + 4, :], in_=picked_rows[24 * q : 24 * (q + 1) : 2, :].bitcast(I32)
-            )
-        load_words(2)
-        load_scales(w4_plane, w4_s)
-        nc.sync.dma_start(out=w4_first[:].bitcast(I32), in_=w4_i[:, 0, :])
-        for g in range(3):
-            load_up(g)
-            load_w4(g)
-
-        v_scales = [v_plane[:].bitcast(U8)[:, S * a : S * (a + 1)] for a in range(PASSES)]
-        w4_bytes = w4_plane[:].bitcast(U8)
+        w4_bytes = w4_plane.bitcast(U8)
+        v_scales = [v_plane.bitcast(U8)[:, S * a : S * (a + 1)] for a in range(PASSES)]
+        windows = [words[i][:, b, :] for i, (a, n) in enumerate(WORD_LOADS) for b in range(n)]
 
         def gather_words(a):
-            nc.vector.tensor_copy(v_codes[a][:], words[a][:].bitcast(U32).indirect(offsets[:]))
-
-        def shared_copy(dst, src, split):
-            if split > 0:
-                nc.vector.tensor_copy(out=dst[:, :split], in_=src[:, :split])
-            if split < dst.shape[1]:
-                nc.scalar.copy(out=dst[:, split:], in_=src[:, split:])
+            nc.vector.tensor_copy(v_codes[a][:], windows[a].bitcast(U32).indirect(offsets[:]))
 
         def group_down(a, split):
             src = d_raw[a][:].rearrange("p j (m u e) -> p u m j e", u=2, e=2)
             dst = d_grp[a][:].rearrange("p (u e) m j -> p u m j e", e=2)
             if split > 0:
                 nc.vector.tensor_copy(out=dst[:, :, :split], in_=src[:, :, :split])
-            nc.scalar.copy(out=dst[:, :, split:], in_=src[:, :, split:])
+            if split < P:
+                nc.scalar.copy(out=dst[:, :, split:], in_=src[:, :, split:])
 
         def quantize_down(a):
             nc.vector.quantize_mx(
@@ -138,12 +164,18 @@ def tile_list_tablora_tm_none_kernel(tc, tab, w4_words, w4_scales, down, up, off
                 in_=d_grp[a][:].rearrange("p t m j -> p (t m j)"),
             )
 
-        def group_up(c, split):
-            g = max(c - 1, 0)
-            first = CHUNK * c - GROUPS[g][0]
-            src = u_raw[g][:, :, first : first + CHUNK].rearrange("p j (c i) -> p c j i", i=4)
+        def group_up(c, on_vector):
+            g, first, width = CHUNKS[c]
+            first += GROUPS[g][0]
+            i = max(i for i, (f, w) in enumerate(UP_LOADS) if f <= first)
+            first -= UP_LOADS[i][0]
+            src = u_raw[i][:, :, first : first + width].rearrange("p j (c i) -> p c j i", i=4)
             dst = u_grp[c][:].rearrange("p (c i) j -> p c j i", i=4)
-            shared_copy(dst, src, split // 4)
+            split = on_vector // 4
+            if split > 0:
+                nc.vector.tensor_copy(out=dst[:, :split], in_=src[:, :split])
+            if on_vector < width:
+                nc.scalar.copy(out=dst[:, split:], in_=src[:, split:])
 
         def quantize_up(c):
             nc.vector.quantize_mx(
@@ -152,21 +184,19 @@ def tile_list_tablora_tm_none_kernel(tc, tab, w4_words, w4_scales, down, up, off
 
         def base(a, g):
             first, width = GROUPS[g]
-            step = N_TILE if width == N_TILE else P
+            step = 512 if width == 512 else P
             for j in range(2):
                 js = slice(P * j, P * (j + 1))
                 for c in range(0, width, step):
-                    if a == 0:
-                        rhs = w4_first[:, 2 * (first + c) : 2 * (first + c + step)]
-                    else:
-                        rhs = w4_rest[g][:, a - 1, 2 * c : 2 * (c + step)]
+                    i = [i for i, (b, n, f, w) in enumerate(W4_LOADS) if b <= a < b + n and f <= first + c < f + w][0]
+                    inside = first + c - W4_LOADS[i][2]
                     nc.tensor.matmul_mx(
-                        out=o_ps[j][g][:, c : c + step],
+                        out=o_ps[g][j][:, c : c + step],
                         lhsT=v_codes[a][:, js].bitcast(FP8X4),
                         lhsT_scale=v_scales[a][:, js],
-                        rhs=rhs.bitcast(FP4X4),
+                        rhs=w4_sb[i][:, a - W4_LOADS[i][0], 2 * inside : 2 * (inside + step)].bitcast(FP4X4),
                         rhs_scale=w4_bytes[:, a * M + first + c : a * M + first + c + step],
-                        start=(a == 0 and c == 0),
+                        start=(a == 0 and c == 0 and (j == 0 or g in SPLIT_BANKS)),
                         stop=False,
                     )
 
@@ -185,12 +215,14 @@ def tile_list_tablora_tm_none_kernel(tc, tab, w4_words, w4_scales, down, up, off
                         stop=(a == PASSES - 1 and t == 3),
                     )
 
-        def group_h(j, on_vector):
-            src = h_ps[j][:].rearrange("p t n -> p n t")
+        def move(dst, src, on_vector):
             if on_vector:
-                nc.vector.tensor_copy(out=h_grp[j][:], in_=src)
+                nc.vector.tensor_copy(out=dst, in_=src)
             else:
-                nc.scalar.copy(out=h_grp[j][:], in_=src)
+                nc.scalar.copy(out=dst, in_=src)
+
+        def group_h(j, on_vector):
+            move(h_grp[j][:], h_ps[j][:].rearrange("p t n -> p n t"), on_vector)
 
         def quantize_h(j):
             nc.vector.quantize_mx(
@@ -198,63 +230,35 @@ def tile_list_tablora_tm_none_kernel(tc, tab, w4_words, w4_scales, down, up, off
             )
 
         def close(c):
-            g = max(c - 1, 0)
-            first = CHUNK * c - GROUPS[g][0]
+            g, first, width = CHUNKS[c]
             for j in range(2):
                 nc.tensor.matmul_mx(
-                    out=o_ps[j][g][:, first : first + CHUNK],
+                    out=o_ps[g][j][:, first : first + width],
                     lhsT=h_codes[j][:].bitcast(FP8X4),
                     lhsT_scale=h_scales[j][:],
                     rhs=u_codes[c][:].bitcast(FP8X4),
                     rhs_scale=u_scales[c][:],
                     start=False,
-                    stop=(first + CHUNK == GROUPS[g][1]),
+                    stop=(first + width == GROUPS[g][1] and (j == 1 or g in SPLIT_BANKS)),
                 )
 
-        def store(g, on_vector):
+        def store(g, on_vector, apart):
             first, width = GROUPS[g]
-            for j in range(2):
-                if j in on_vector:
-                    nc.vector.tensor_copy(out=o_sb[j][g][:], in_=o_ps[j][g][:])
-                else:
-                    nc.scalar.copy(out=o_sb[j][g][:], in_=o_ps[j][g][:])
-                nc.sync.dma_start(out=out[P * j : P * (j + 1), first : first + width], in_=o_sb[j][g][:])
+            if g in SPLIT_BANKS:
+                for j in range(2):
+                    move(o_sb[g][:, j, :], o_ps[g][j], j in on_vector)
+                    if apart:
+                        nc.sync.dma_start(out=out_v[:, j, first : first + width], in_=o_sb[g][:, j, :])
+            else:
+                move(o_sb[g][:], o_ps[g][2], 0 in on_vector)
+            if not apart:
+                nc.sync.dma_start(out=out_v[:, :, first : first + width], in_=o_sb[g][:])
 
-        group_down(0, 0)
-        quantize_down(0)
-        gather_words(0)
-        low_rank(0)
-        group_down(1, 0)
-        gather_words(1)
-        quantize_down(1)
-        low_rank(1)
-        group_down(2, D_SPLIT)
-        quantize_down(2)
-        gather_words(2)
-        low_rank(2)
-        group_h(0, False)
-        group_h(1, True)
-        quantize_h(0)
-        quantize_h(1)
-        for g in range(3):
-            base(0, g)
-        group_up(0, U_SPLIT)
-        group_up(1, U_SPLIT)
-        base(1, 0)
-        base(2, 0)
-        for c in range(2):
-            quantize_up(c)
-            close(c)
-        group_up(2, U_SPLIT)
-        store(0, ())
-        base(1, 1)
-        base(2, 1)
-        quantize_up(2)
-        close(2)
-        group_up(3, CHUNK)
-        store(1, ())
-        base(1, 2)
-        base(2, 2)
-        quantize_up(3)
-        close(3)
-        store(2, (1,))
+        calls = {
+            "list": load_list, "down": load_down, "words": load_words, "w4": load_w4, "up": load_up,
+            "ts": load_tab_scales, "gs": gather_scales, "ws": load_w4_scales, "mv": move_scales,
+            "gw": gather_words, "gd": group_down, "qd": quantize_down, "gu": group_up, "qu": quantize_up,
+            "base": base, "lr": low_rank, "gh": group_h, "qh": quantize_h, "close": close, "store": store,
+        }
+        for step in LOADS + STEPS:
+            calls[step[0]](*step[1:])

@@ -16,15 +16,17 @@ FP4X4 = mybir.dt.float4_e2m1fn_x4
 
 P = 128
 PASSES = K // 512
-GROUPS = ((0, 512), (512, 256), (768, 128), (896, 128))
-CHUNKS = ((0, 0, 256), (0, 256, 256), (1, 0, 256), (2, 0, 128), (3, 0, 128))
-UP_LOADS = ((0, 512), (512, 256), (768, 128), (896, 128))
-W4_LOADS = ((0, 3, 0, 512), (0, 3, 512, 384), (0, 3, 896, 128))
-WORD_LOADS = ((0, 2), (2, 1))
+GROUPS = ((0, 256), (256, 256), (512, 256), (768, 256))
+CHUNKS = ((0, 0, 256), (1, 0, 256), (2, 0, 256), (3, 0, 256))
+UP_LOADS = ((0, 1024),)
+W4_LOADS = ((0, 1, 0, 1024), (1, 1, 0, 1024), (2, 1, 0, 1024))
+WORD_LOADS = ((0, 1), (1, 1), (2, 1))
 SPLIT_BANKS = (0, 3)
-LOADS = (('down', 0), ('list',), ('ts', 'sync'), ('ws', 'sync'), ('gs',), ('down', 1), ('words', 0), ('down', 2), ('mv', 'sync'), ('words', 1), ('w4', 0), ('up', 0), ('w4', 1), ('up', 1), ('up', 2), ('up', 3), ('w4', 2))
-STEPS = (('gd', 0, 0), ('qd', 0), ('gw', 0), ('lr', 0), ('gd', 1, 0), ('gw', 1), ('qd', 1), ('lr', 1), ('gd', 2, 88), ('qd', 2), ('gw', 2), ('lr', 2), ('gh', 0, 0), ('gh', 1, 1), ('qh', 0), ('qh', 1), ('base', 0, 0), ('base', 1, 0), ('base', 2, 0), ('gu', 0, 176), ('gu', 1, 176), ('qu', 0), ('close', 0), ('qu', 1), ('close', 1), ('base', 0, 1), ('base', 1, 1), ('base', 2, 1), ('base', 0, 2), ('base', 1, 2), ('base', 2, 2), ('gu', 2, 176), ('store', 0, (), 1), ('qu', 2), ('close', 2), ('gu', 3, 128), ('qu', 3), ('store', 1, (), 0), ('close', 3), ('gu', 4, 128), ('base', 0, 3), ('base', 1, 3), ('base', 2, 3), ('qu', 4), ('store', 2, (), 0), ('close', 4), ('store', 3, (1,), 0))
-MERGED = True
+LOADS = (('down', 0), ('list',), ('ts', 'sync'), ('ws', 'sync'), ('gs',), ('down', 1), ('words', 0), ('words', 1), ('down', 2), ('words', 2), ('w4', 0), ('mv', 'sync'), ('up', 0), ('w4', 1), ('w4', 2))
+STEPS = (('gd', 0, 0), ('qd', 0), ('gw', 0), ('gd', 1, 0), ('gw', 1), ('qd', 1), ('gw', 2), ('gd', 2, 88), ('qd', 2), ('lr', 0), ('lr', 1), ('lr', 2), ('gh', 0, 0), ('gh', 1, 1), ('qh', 0), ('qh', 1), ('base', 0, 0), ('base', 0, 1), ('base', 0, 2), ('base', 0, 3), ('gu', 0, 144), ('qu', 0), ('gu', 1, 208), ('base', 1, 0), ('base', 2, 0), ('close', 0), ('gu', 2, 128), ('qu', 1), ('store', 0, (1,), 1), ('base', 1, 1), ('base', 2, 1), ('qu', 2), ('close', 1), ('gu', 3, 160), ('store', 1, (), 0), ('base', 1, 2), ('base', 2, 2), ('qu', 3), ('close', 2), ('base', 1, 3), ('base', 2, 3), ('close', 3), ('store', 2, (0,), 0), ('store', 3, (1,), 0))
+MODE = 'merged'
+JSPLIT = False
+MERGED = MODE == "merged"
 WORD_COLS = 512 * T // 4
 W4_COLS = PASSES * M // 4
 ROW0, STEP = 32, 4
@@ -39,8 +41,8 @@ def tile_list_tablora_tm_none_kernel(tc, tab, w4_words, w4_scales, down, up, off
 
         offsets = keep.tile([P, S // 16], U16, name="offsets")
         words = [keep.tile([P, n, T], I32, name=f"words{a}", align_bytes=64) for a, n in WORD_LOADS]
-        tab_rows = keep.tile([P, PASSES * T // 4], I32, name="tab_rows", align_bytes=64)
-        picked_rows = keep.tile([P, PASSES * S], U8, name="picked_rows", align_bytes=64)
+        tab_rows = keep.tile([P, (1 if MODE == "one" else PASSES) * T // 4], I32, name="tab_rows", align_bytes=64)
+        picked_rows = keep.tile([P, (1 if MODE == "one" else PASSES) * S], U8, name="picked_rows", align_bytes=64)
         if MERGED:
             stage = keep.tile([P, W4_COLS + V_COLS], I32, name="stage", align_bytes=64)
             plane = keep.tile([P, W4_COLS + V_COLS], I32, name="plane", align_bytes=64)
@@ -58,7 +60,8 @@ def tile_list_tablora_tm_none_kernel(tc, tab, w4_words, w4_scales, down, up, off
         d_codes = [keep.tile([P, R], U32, name=f"d_codes{a}", align_bytes=64) for a in range(PASSES)]
         d_scales = [keep.tile([P, R], U8, name=f"d_scales{a}", align_bytes=64) for a in range(PASSES)]
         u_raw = [
-            keep.tile([P, 4, width], F32, name=f"u_raw{g}", align_bytes=64) for g, (first, width) in enumerate(UP_LOADS)
+            keep.tile([P, 2 if JSPLIT else 4, width], F32, name=f"u_raw{g}", align_bytes=64)
+            for g, (first, width) in enumerate(UP_LOADS)
         ]
         u_grp = [keep.tile([P, w, 4], BF16, name=f"u_grp{c}", align_bytes=64) for c, (g, f, w) in enumerate(CHUNKS)]
         u_codes = [keep.tile([P, w], U32, name=f"u_codes{c}", align_bytes=64) for c, (g, f, w) in enumerate(CHUNKS)]
@@ -83,7 +86,8 @@ def tile_list_tablora_tm_none_kernel(tc, tab, w4_words, w4_scales, down, up, off
         if MERGED:
             nc.vector.memset(plane[:], 0)
         else:
-            nc.vector.memset(v_plane, 0)
+            if MODE != "direct":
+                nc.vector.memset(v_plane, 0)
             nc.vector.memset(w4_plane, 0)
         tab_i = tab.bitcast(I32)
         tab_s = tab_i[:, WORD_COLS:].rearrange("a (q t) -> q a t", q=16)
@@ -110,14 +114,27 @@ def tile_list_tablora_tm_none_kernel(tc, tab, w4_words, w4_scales, down, up, off
 
         def load_up(i):
             first, width = UP_LOADS[i]
-            nc.sync.dma_start(out=u_raw[i][:], in_=up_v[:, :, first : first + width])
+            if JSPLIT:
+                nc.sync.dma_start(out=u_raw[i][:], in_=up_v[:, 2 * i : 2 * i + 2, :])
+            else:
+                nc.sync.dma_start(out=u_raw[i][:], in_=up_v[:, :, first : first + width])
 
         def load_tab_scales(queue):
+            if MODE == "one":
+                queues[queue].dma_start(out=tab_rows[0:96:2, :], in_=tab_s)
+                return
+            if MODE == "direct":
+                rows = tab_i[:, WORD_COLS:].rearrange("a (q r t) -> r q a t", q=4, r=4)
+                for r in range(4):
+                    queues[queue].dma_start(
+                        out=tab_rows[r:P:32, :].rearrange("q (a t) -> q a t", a=PASSES), in_=rows[r]
+                    )
+                return
             queues[queue].dma_start(out=tab_rows[ROW0 : ROW0 + 16 * STEP - STEP + 1 : STEP, :].rearrange("q (a t) -> q a t", a=PASSES), in_=tab_s)
 
         def gather_scales():
             tab_bytes = tab_rows[:].bitcast(U8)
-            for a in range(PASSES):
+            for a in range(1 if MODE == "one" else PASSES):
                 nc.vector.tensor_copy(
                     picked_rows[:, S * a : S * (a + 1)], tab_bytes[:, T * a : T * (a + 1)].indirect(offsets[:])
                 )
@@ -137,12 +154,18 @@ def tile_list_tablora_tm_none_kernel(tc, tab, w4_words, w4_scales, down, up, off
 
         def move_scales(queue):
             for r in range(4):
-                if MERGED:
+                if MODE == "one":
+                    queues[queue].dma_start(
+                        out=v_plane[32 * r : 32 * r + 4, :], in_=picked_rows[24 * r : 24 * (r + 1) : 2, :].bitcast(I32)
+                    )
+                elif MERGED:
                     queues[queue].dma_start(out=plane[r:P:32, :], in_=stage[ROW0 + STEP * r : ROW0 + STEP * (r + 12) + 1 : 4 * STEP, :])
                 else:
                     queues[queue].dma_start(out=v_plane[r:P:32, :], in_=picked_rows[ROW0 + STEP * r : ROW0 + STEP * (r + 12) + 1 : 4 * STEP, :].bitcast(I32))
 
         w4_bytes = w4_plane.bitcast(U8)
+        if MODE == "direct":
+            v_plane = picked_rows[:].bitcast(I32)
         v_scales = [v_plane.bitcast(U8)[:, S * a : S * (a + 1)] for a in range(PASSES)]
         windows = [words[i][:, b, :] for i, (a, n) in enumerate(WORD_LOADS) for b in range(n)]
 
@@ -164,9 +187,18 @@ def tile_list_tablora_tm_none_kernel(tc, tab, w4_words, w4_scales, down, up, off
                 in_=d_grp[a][:].rearrange("p t m j -> p (t m j)"),
             )
 
-        def group_up(c, on_vector):
+        def group_up(c, on_vector, half=1):
             g, first, width = CHUNKS[c]
             first += GROUPS[g][0]
+            if JSPLIT:
+                src = u_raw[half][:, :, first : first + width].rearrange("p j (c i) -> p c j i", i=4)
+                dst = u_grp[c][:, :, 2 * half : 2 * half + 2].rearrange("p (c i) j -> p c j i", i=4)
+                split = on_vector // 4
+                if split > 0:
+                    nc.vector.tensor_copy(out=dst[:, :split], in_=src[:, :split])
+                if on_vector < width:
+                    nc.scalar.copy(out=dst[:, split:], in_=src[:, split:])
+                return
             i = max(i for i, (f, w) in enumerate(UP_LOADS) if f <= first)
             first -= UP_LOADS[i][0]
             src = u_raw[i][:, :, first : first + width].rearrange("p j (c i) -> p c j i", i=4)
@@ -182,7 +214,7 @@ def tile_list_tablora_tm_none_kernel(tc, tab, w4_words, w4_scales, down, up, off
                 out=u_codes[c][:].bitcast(FP8X4), scales=u_scales[c][:], in_=u_grp[c][:].rearrange("p w j -> p (w j)")
             )
 
-        def base(a, g):
+        def base(a, g, last=0):
             first, width = GROUPS[g]
             step = 512 if width == 512 else P
             for j in range(2):
@@ -197,7 +229,7 @@ def tile_list_tablora_tm_none_kernel(tc, tab, w4_words, w4_scales, down, up, off
                         rhs=w4_sb[i][:, a - W4_LOADS[i][0], 2 * inside : 2 * (inside + step)].bitcast(FP4X4),
                         rhs_scale=w4_bytes[:, a * M + first + c : a * M + first + c + step],
                         start=(a == 0 and c == 0 and (j == 0 or g in SPLIT_BANKS)),
-                        stop=False,
+                        stop=(last == 1 and c + step == width and (j == 1 or g in SPLIT_BANKS)),
                     )
 
         def low_rank(a):
@@ -229,7 +261,7 @@ def tile_list_tablora_tm_none_kernel(tc, tab, w4_words, w4_scales, down, up, off
                 out=h_codes[j][:].bitcast(FP8X4), scales=h_scales[j][:], in_=h_grp[j][:].rearrange("p w j -> p (w j)")
             )
 
-        def close(c):
+        def close(c, may_stop=1):
             g, first, width = CHUNKS[c]
             for j in range(2):
                 nc.tensor.matmul_mx(
@@ -239,7 +271,7 @@ def tile_list_tablora_tm_none_kernel(tc, tab, w4_words, w4_scales, down, up, off
                     rhs=u_codes[c][:].bitcast(FP8X4),
                     rhs_scale=u_scales[c][:],
                     start=False,
-                    stop=(first + width == GROUPS[g][1] and (j == 1 or g in SPLIT_BANKS)),
+                    stop=(may_stop == 1 and first + width == GROUPS[g][1] and (j == 1 or g in SPLIT_BANKS)),
                 )
 
         def store(g, on_vector, apart):
@@ -257,7 +289,7 @@ def tile_list_tablora_tm_none_kernel(tc, tab, w4_words, w4_scales, down, up, off
         calls = {
             "list": load_list, "down": load_down, "words": load_words, "w4": load_w4, "up": load_up,
             "ts": load_tab_scales, "gs": gather_scales, "ws": load_w4_scales, "mv": move_scales,
-            "gw": gather_words, "gd": group_down, "qd": quantize_down, "gu": group_up, "qu": quantize_up,
+            "ga": lambda c, on_vector: group_up(c, on_vector, 0), "gw": gather_words, "gd": group_down, "qd": quantize_down, "gu": group_up, "qu": quantize_up,
             "base": base, "lr": low_rank, "gh": group_h, "qh": quantize_h, "close": close, "store": store,
         }
         for step in LOADS + STEPS:

@@ -16,14 +16,14 @@ FP4X4 = mybir.dt.float4_e2m1fn_x4
 
 P = 128
 PASSES = K // 512
-GROUPS = ((0, 256), (256, 256), (512, 256), (768, 256))
-CHUNKS = ((0, 0, 256), (1, 0, 256), (2, 0, 256), (3, 0, 256))
-UP_LOADS = ((0, 1024),)
+GROUPS = ((0, 512), (512, 256), (768, 256))
+CHUNKS = ((0, 0, 256), (0, 256, 256), (1, 0, 256), (2, 0, 256))
+UP_LOADS = ((0, 512), (512, 256), (768, 256))
 W4_LOADS = ((0, 1, 0, 1024), (1, 1, 0, 1024), (2, 1, 0, 1024))
 WORD_LOADS = ((0, 1), (1, 1), (2, 1))
-SPLIT_BANKS = (0, 3)
-LOADS = (('down', 0), ('list',), ('ts', 'sync'), ('ws', 'sync'), ('gs',), ('down', 1), ('words', 0), ('words', 1), ('down', 2), ('words', 2), ('w4', 0), ('mv', 'sync'), ('up', 0), ('w4', 1), ('w4', 2))
-STEPS = (('gd', 0, 0), ('qd', 0), ('gw', 0), ('gd', 1, 0), ('gw', 1), ('qd', 1), ('gw', 2), ('gd', 2, 88), ('qd', 2), ('lr', 0), ('lr', 1), ('lr', 2), ('gh', 0, 0), ('gh', 1, 1), ('qh', 0), ('qh', 1), ('base', 0, 0), ('base', 0, 1), ('base', 0, 2), ('base', 0, 3), ('gu', 0, 144), ('qu', 0), ('gu', 1, 208), ('base', 1, 0), ('base', 2, 0), ('close', 0), ('gu', 2, 128), ('qu', 1), ('store', 0, (1,), 1), ('base', 1, 1), ('base', 2, 1), ('qu', 2), ('close', 1), ('gu', 3, 160), ('store', 1, (), 0), ('base', 1, 2), ('base', 2, 2), ('qu', 3), ('close', 2), ('base', 1, 3), ('base', 2, 3), ('close', 3), ('store', 2, (0,), 0), ('store', 3, (1,), 0))
+SPLIT_BANKS = (0, 1, 2)
+LOADS = (('down', 0), ('list',), ('ts', 'sync'), ('ws', 'sync'), ('gs',), ('down', 1), ('words', 0), ('words', 1), ('down', 2), ('mv', 'sync'), ('words', 2), ('w4', 0), ('up', 0), ('w4', 1), ('w4', 2), ('up', 1), ('up', 2))
+STEPS = (('gd', 0, 0), ('qd', 0), ('gw', 0), ('lr', 0), ('gd', 1, 0), ('gw', 1), ('qd', 1), ('lr', 1), ('gd', 2, 88), ('qd', 2), ('gw', 2), ('lr', 2), ('gh', 0, 0), ('gh', 1, 1), ('qh', 0), ('qh', 1), ('base', 0, 0), ('base', 0, 1), ('base', 0, 2), ('gu', 0, 176), ('gu', 1, 176), ('base', 1, 0), ('base', 2, 0), ('qu', 0), ('close', 0), ('qu', 1), ('close', 1), ('store', 0, (), 1), ('base', 1, 1), ('base', 2, 1), ('gu', 2, 256), ('qu', 2), ('close', 2), ('base', 1, 2), ('base', 2, 2), ('gu', 3, 176), ('qu', 3), ('store', 1, (), 0), ('close', 3), ('store', 2, (1,), 1))
 MODE = 'merged'
 JSPLIT = False
 MERGED = MODE == "merged"

@@ -17,13 +17,13 @@ FP4X4 = mybir.dt.float4_e2m1fn_x4
 P = 128
 PASSES = K // 512
 GROUPS = ((0, 512), (512, 256), (768, 256))
-CHUNKS = ((0, 0, 256), (0, 256, 256), (1, 0, 256), (2, 0, 256))
+CHUNKS = ((0, 0, 256), (0, 256, 256), (1, 0, 256), (2, 0, 128), (2, 128, 128))
 UP_LOADS = ((0, 512), (512, 256), (768, 256))
 W4_LOADS = ((0, 1, 0, 1024), (1, 1, 0, 1024), (2, 1, 0, 1024))
 WORD_LOADS = ((0, 1), (1, 1), (2, 1))
 SPLIT_BANKS = (0, 1, 2)
 LOADS = (('down', 0), ('list',), ('ts', 'sync'), ('ws', 'sync'), ('gs',), ('down', 1), ('words', 0), ('words', 1), ('down', 2), ('mv', 'sync'), ('words', 2), ('w4', 0), ('up', 0), ('w4', 1), ('w4', 2), ('up', 1), ('up', 2))
-STEPS = (('gd', 0, 0), ('qd', 0), ('gw', 0), ('lr', 0), ('gd', 1, 0), ('gw', 1), ('qd', 1), ('lr', 1), ('gd', 2, 88), ('qd', 2), ('gw', 2), ('lr', 2), ('gh', 0, 0), ('gh', 1, 1), ('qh', 0), ('qh', 1), ('base', 0, 0), ('base', 0, 1), ('base', 0, 2), ('gu', 0, 176), ('gu', 1, 176), ('base', 1, 0), ('base', 2, 0), ('qu', 0), ('close', 0), ('qu', 1), ('close', 1), ('store', 0, (), 1), ('base', 1, 1), ('base', 2, 1), ('gu', 2, 256), ('qu', 2), ('close', 2), ('base', 1, 2), ('base', 2, 2), ('gu', 3, 176), ('qu', 3), ('store', 1, (), 0), ('close', 3), ('store', 2, (1,), 1))
+STEPS = (('gd', 0, 0), ('qd', 0), ('gw', 0), ('lr', 0), ('gd', 1, 0), ('gw', 1), ('qd', 1), ('lr', 1), ('gd', 2, 88), ('qd', 2), ('gw', 2), ('lr', 2), ('gh', 0, 0), ('gh', 1, 1), ('qh', 0), ('qh', 1), ('base', 0, 0), ('base', 0, 1), ('base', 0, 2), ('gu', 0, 176), ('gu', 1, 176), ('base', 1, 0), ('base', 2, 0), ('qu', 0), ('close', 0), ('qu', 1), ('close', 1), ('store', 0, (), 1), ('base', 1, 1), ('base', 2, 1), ('gu', 2, 256), ('qu', 2), ('close', 2), ('base', 1, 2), ('base', 2, 2), ('gu', 3, 128), ('gu', 4, 48), ('qu', 3), ('close', 3), ('qu', 4), ('store', 1, (), 0), ('close', 4), ('store', 2, (1,), 1))
 MODE = 'merged'
 JSPLIT = False
 MERGED = MODE == "merged"

@@ -22,8 +22,8 @@ UP_LOADS = ((0, 512), (512, 256), (768, 256))
 W4_LOADS = ((0, 1, 0, 1024), (1, 1, 0, 1024), (2, 1, 0, 1024))
 WORD_LOADS = ((0, 1), (1, 1), (2, 1))
 SPLIT_BANKS = (0, 1, 2)
-LOADS = (('down', 0), ('list',), ('ts', 'sync'), ('ws', 'sync'), ('gs',), ('down', 1), ('words', 0), ('words', 1), ('down', 2), ('mv', 'sync'), ('words', 2), ('w4', 0), ('up', 0), ('w4', 1), ('w4', 2), ('up', 1), ('up', 2))
-STEPS = (('gd', 0, 0), ('qd', 0), ('gw', 0), ('lr', 0), ('gd', 1, 0), ('gw', 1), ('qd', 1), ('lr', 1), ('gd', 2, 88), ('qd', 2), ('gw', 2), ('lr', 2), ('gh', 0, 0), ('gh', 1, 1), ('qh', 0), ('qh', 1), ('base', 0, 0), ('base', 0, 1), ('base', 0, 2), ('gu', 0, 176), ('gu', 1, 176), ('base', 1, 0), ('base', 2, 0), ('qu', 0), ('close', 0), ('qu', 1), ('close', 1), ('store', 0, (), 1), ('base', 1, 1), ('base', 2, 1), ('gu', 2, 256), ('qu', 2), ('close', 2), ('base', 1, 2), ('base', 2, 2), ('gu', 3, 128), ('gu', 4, 48), ('qu', 3), ('close', 3), ('qu', 4), ('store', 1, (), 0), ('close', 4), ('store', 2, (1,), 1))
+LOADS = (('down', 0), ('list',), ('ts', 'sync'), ('ws', 'sync'), ('gs',), ('down', 1), ('words', 0), ('down', 2), ('mv', 'sync'), ('words', 1), ('words', 2), ('w4', 0), ('up', 0), ('w4', 1), ('w4', 2), ('up', 1), ('up', 2))
+STEPS = (('gd', 0, 0), ('qd', 0), ('gw', 0), ('gd', 1, 0), ('qd', 1), ('lr', 0), ('gd', 2, 88), ('qd', 2), ('gw', 1), ('lr', 1), ('gw', 2), ('lr', 2), ('gh', 0, 0), ('gh', 1, 1), ('qh', 0), ('qh', 1), ('base', 0, 0), ('base', 0, 1), ('base', 0, 2), ('gu', 0, 160), ('gu', 1, 160), ('base', 1, 0), ('base', 2, 0), ('qu', 0), ('close', 0), ('qu', 1), ('close', 1), ('store', 0, (), 1), ('base', 1, 1), ('base', 2, 1), ('gu', 2, 256), ('qu', 2), ('close', 2), ('base', 1, 2), ('base', 2, 2), ('gu', 3, 80), ('gu', 4, 96), ('qu', 3), ('close', 3), ('qu', 4), ('store', 1, (), 0), ('close', 4), ('store', 2, (1,), 1))
 MODE = 'merged'
 JSPLIT = False
 MERGED = MODE == "merged"
@@ -115,7 +115,8 @@ def tile_list_tablora_tm_none_kernel(tc, tab, w4_words, w4_scales, down, up, off
         def load_up(i):
             first, width = UP_LOADS[i]
             if JSPLIT:
-                nc.sync.dma_start(out=u_raw[i][:], in_=up_v[:, 2 * i : 2 * i + 2, :])
+                half = min(i, 1)
+                nc.sync.dma_start(out=u_raw[i][:], in_=up_v[:, 2 * half : 2 * half + 2, first : first + width])
             else:
                 nc.sync.dma_start(out=u_raw[i][:], in_=up_v[:, :, first : first + width])
 
@@ -191,7 +192,9 @@ def tile_list_tablora_tm_none_kernel(tc, tab, w4_words, w4_scales, down, up, off
             g, first, width = CHUNKS[c]
             first += GROUPS[g][0]
             if JSPLIT:
-                src = u_raw[half][:, :, first : first + width].rearrange("p j (c i) -> p c j i", i=4)
+                i = half * max(i for i, (f, w) in enumerate(UP_LOADS) if f <= first)
+                first -= UP_LOADS[i][0]
+                src = u_raw[i][:, :, first : first + width].rearrange("p j (c i) -> p c j i", i=4)
                 dst = u_grp[c][:, :, 2 * half : 2 * half + 2].rearrange("p (c i) j -> p c j i", i=4)
                 split = on_vector // 4
                 if split > 0:

@@ -16,21 +16,19 @@ FP4X4 = mybir.dt.float4_e2m1fn_x4
 
 P = 128
 PASSES = K // 512
-GROUPS = ((0, 512), (512, 256), (768, 256))
-CHUNKS = ((0, 0, 256), (0, 256, 256), (1, 0, 256), (2, 0, 128), (2, 128, 128))
-UP_LOADS = ((0, 512), (512, 256), (768, 256))
-W4_LOADS = ((0, 1, 0, 1024), (1, 1, 0, 1024), (2, 1, 0, 1024))
-WORD_LOADS = ((0, 1), (1, 1), (2, 1))
-SPLIT_BANKS = (0, 1, 2)
-LOADS = (('down', 0), ('list',), ('ts', 'sync'), ('ws', 'sync'), ('gs',), ('down', 1), ('words', 0), ('down', 2), ('mv', 'sync'), ('words', 1), ('words', 2), ('w4', 0), ('up', 0), ('w4', 1), ('w4', 2), ('up', 1), ('up', 2))
-STEPS = (('gd', 0, 0), ('qd', 0), ('gw', 0), ('gd', 1, 0), ('qd', 1), ('lr', 0), ('gd', 2, 88), ('qd', 2), ('gw', 1), ('lr', 1), ('gw', 2), ('lr', 2), ('gh', 0, 0), ('gh', 1, 1), ('qh', 0), ('qh', 1), ('base', 0, 0), ('base', 0, 1), ('base', 0, 2), ('gu', 0, 160), ('gu', 1, 160), ('base', 1, 0), ('base', 2, 0), ('qu', 0), ('close', 0), ('qu', 1), ('close', 1), ('store', 0, (), 1), ('base', 1, 1), ('base', 2, 1), ('gu', 2, 256), ('qu', 2), ('close', 2), ('base', 1, 2), ('base', 2, 2), ('gu', 3, 80), ('gu', 4, 96), ('qu', 3), ('close', 3), ('qu', 4), ('store', 1, (), 0), ('close', 4), ('store', 2, (1,), 1))
-MODE = 'merged'
-JSPLIT = False
-MERGED = MODE == "merged"
+BLOCKS = 16
+BANK = 512
 WORD_COLS = 512 * T // 4
 W4_COLS = PASSES * M // 4
-ROW0, STEP = 32, 4
 V_COLS = PASSES * S // 4
+
+ROW0, STEP = 32, 4
+STAGED = slice(ROW0, ROW0 + STEP * (BLOCKS - 1) + 1, STEP)
+
+GROUPS = ((0, 512), (512, 256), (768, 256))
+CHUNKS = ((0, 0, 256), (0, 256, 256), (1, 0, 256), (2, 0, 128), (2, 128, 128))
+UP_ON_VECTOR = (160, 160, 256, 80, 96)
+DOWN_ON_VECTOR = (0, 0, 88)
 
 
 def tile_list_tablora_tm_none_kernel(tc, tab, w4_words, w4_scales, down, up, offs, out):
@@ -39,232 +37,152 @@ def tile_list_tablora_tm_none_kernel(tc, tab, w4_words, w4_scales, down, up, off
         keep = ctx.enter_context(tc.tile_pool(name="keep", bufs=1))
         psum = ctx.enter_context(tc.psum_pool(name="psum", bufs=1))
 
+        def sbuf(name, shape, dtype):
+            return keep.tile(shape, dtype, name=name, align_bytes=64)
+
         offsets = keep.tile([P, S // 16], U16, name="offsets")
-        words = [keep.tile([P, n, T], I32, name=f"words{a}", align_bytes=64) for a, n in WORD_LOADS]
-        tab_rows = keep.tile([P, (1 if MODE == "one" else PASSES) * T // 4], I32, name="tab_rows", align_bytes=64)
-        picked_rows = keep.tile([P, (1 if MODE == "one" else PASSES) * S], U8, name="picked_rows", align_bytes=64)
-        if MERGED:
-            stage = keep.tile([P, W4_COLS + V_COLS], I32, name="stage", align_bytes=64)
-            plane = keep.tile([P, W4_COLS + V_COLS], I32, name="plane", align_bytes=64)
-            w4_plane = plane[:, :W4_COLS]
-            v_plane = plane[:, W4_COLS:]
-        else:
-            w4_plane = keep.tile([P, W4_COLS], I32, name="w4_plane", align_bytes=64)[:]
-            v_plane = keep.tile([P, V_COLS], I32, name="v_plane", align_bytes=64)[:]
-        w4_sb = [
-            keep.tile([P, n, 2 * width], U8, name=f"w4_sb{i}", align_bytes=64)
-            for i, (a, n, first, width) in enumerate(W4_LOADS)
-        ]
-        d_raw = [keep.tile([P, 4, R], F32, name=f"d_raw{a}", align_bytes=64) for a in range(PASSES)]
-        d_grp = [keep.tile([P, 4, P, 4], BF16, name=f"d_grp{a}", align_bytes=64) for a in range(PASSES)]
-        d_codes = [keep.tile([P, R], U32, name=f"d_codes{a}", align_bytes=64) for a in range(PASSES)]
-        d_scales = [keep.tile([P, R], U8, name=f"d_scales{a}", align_bytes=64) for a in range(PASSES)]
-        u_raw = [
-            keep.tile([P, 2 if JSPLIT else 4, width], F32, name=f"u_raw{g}", align_bytes=64)
-            for g, (first, width) in enumerate(UP_LOADS)
-        ]
-        u_grp = [keep.tile([P, w, 4], BF16, name=f"u_grp{c}", align_bytes=64) for c, (g, f, w) in enumerate(CHUNKS)]
-        u_codes = [keep.tile([P, w], U32, name=f"u_codes{c}", align_bytes=64) for c, (g, f, w) in enumerate(CHUNKS)]
-        u_scales = [keep.tile([P, w], U8, name=f"u_scales{c}", align_bytes=64) for c, (g, f, w) in enumerate(CHUNKS)]
-        v_codes = [keep.tile([P, S], U32, name=f"v_codes{a}", align_bytes=64) for a in range(PASSES)]
-        h_grp = [keep.tile([P, P, 4], BF16, name=f"h_grp{j}", align_bytes=64) for j in range(2)]
-        h_codes = [keep.tile([P, P], U32, name=f"h_codes{j}", align_bytes=64) for j in range(2)]
-        h_scales = [keep.tile([P, P], U8, name=f"h_scales{j}", align_bytes=64) for j in range(2)]
-        o_sb = [
-            keep.tile([P, 2, width], F32, name=f"o_sb{g}", align_bytes=64) for g, (first, width) in enumerate(GROUPS)
-        ]
+        words = [sbuf(f"words{a}", [P, T], I32) for a in range(PASSES)]
+        tab_rows = sbuf("tab_rows", [P, PASSES * T // 4], I32)
+        picked_rows = sbuf("picked_rows", [P, PASSES * S], U8)
+        stage = sbuf("stage", [P, W4_COLS + V_COLS], I32)
+        plane = sbuf("plane", [P, W4_COLS + V_COLS], I32)
+        w4_sb = [sbuf(f"w4_sb{a}", [P, 2 * M], U8) for a in range(PASSES)]
+        d_raw = [sbuf(f"d_raw{a}", [P, 4, R], F32) for a in range(PASSES)]
+        d_grp = [sbuf(f"d_grp{a}", [P, 4, P, 4], BF16) for a in range(PASSES)]
+        d_codes = [sbuf(f"d_codes{a}", [P, R], U32) for a in range(PASSES)]
+        d_scales = [sbuf(f"d_scales{a}", [P, R], U8) for a in range(PASSES)]
+        u_raw = [sbuf(f"u_raw{g}", [P, 4, width], F32) for g, (first, width) in enumerate(GROUPS)]
+        u_grp = [sbuf(f"u_grp{c}", [P, width, 4], BF16) for c, (g, first, width) in enumerate(CHUNKS)]
+        u_codes = [sbuf(f"u_codes{c}", [P, width], U32) for c, (g, first, width) in enumerate(CHUNKS)]
+        u_scales = [sbuf(f"u_scales{c}", [P, width], U8) for c, (g, first, width) in enumerate(CHUNKS)]
+        v_codes = [sbuf(f"v_codes{a}", [P, S], U32) for a in range(PASSES)]
+        h_grp = [sbuf(f"h_grp{j}", [P, P, 4], BF16) for j in range(2)]
+        h_codes = [sbuf(f"h_codes{j}", [P, P], U32) for j in range(2)]
+        h_scales = [sbuf(f"h_scales{j}", [P, P], U8) for j in range(2)]
+        o_sb = [sbuf(f"o_sb{g}", [P, 2, width], F32) for g, (first, width) in enumerate(GROUPS)]
         h_ps = [psum.tile([P, 4, P], F32, name=f"h_ps{j}") for j in range(2)]
-        o_ps = []
-        for g, (first, width) in enumerate(GROUPS):
-            if g in SPLIT_BANKS:
-                o_ps.append([psum.tile([P, width], F32, name=f"o_ps{g}{j}")[:] for j in range(2)])
-            else:
-                both = psum.tile([P, 2, width], F32, name=f"o_ps{g}")
-                o_ps.append([both[:, 0, :], both[:, 1, :], both[:]])
+        o_ps = [
+            [psum.tile([P, width], F32, name=f"o_ps{g}{j}") for j in range(2)] for g, (first, width) in enumerate(GROUPS)
+        ]
 
-        nc.vector.memset(tab_rows[:], 0)
-        if MERGED:
-            nc.vector.memset(plane[:], 0)
-        else:
-            if MODE != "direct":
-                nc.vector.memset(v_plane, 0)
-            nc.vector.memset(w4_plane, 0)
         tab_i = tab.bitcast(I32)
-        tab_s = tab_i[:, WORD_COLS:].rearrange("a (q t) -> q a t", q=16)
-        w4_i = w4_words.bitcast(I32).rearrange("a p n -> p a n")
-        up_v = up.rearrange("(p j) n -> p j n", j=4)
+        w4_i = w4_words.bitcast(I32)
+        up_v = up.rearrange("(p t) n -> p t n", t=4)
         out_v = out.rearrange("(j p) n -> p j n", j=2)
-        queues = {"sync": nc.sync, "scalar": nc.scalar, "gpsimd": nc.gpsimd}
-
-        def load_list():
-            nc.sync.dma_start(offsets[:], offs)
+        w4_plane = plane[:, :W4_COLS].bitcast(U8)
+        v_planes = [plane[:, W4_COLS:].bitcast(U8)[:, S * a : S * (a + 1)] for a in range(PASSES)]
 
         def load_down(a):
             nc.sync.dma_start(
-                out=d_raw[a][:], in_=down[512 * a : 512 * (a + 1), :].rearrange("(p j) r -> p j r", j=4)
+                out=d_raw[a][:], in_=down[512 * a : 512 * (a + 1), :].rearrange("(p t) r -> p t r", t=4)
             )
 
-        def load_words(i):
-            a, n = WORD_LOADS[i]
-            nc.sync.dma_start(out=words[i][:], in_=tab_i[a : a + n, :WORD_COLS].rearrange("a (p t) -> p a t", p=P))
+        def load_words(a):
+            nc.sync.dma_start(out=words[a][:], in_=tab_i[a, :WORD_COLS].rearrange("(p c) -> p c", p=P))
 
-        def load_w4(i):
-            a, n, first, width = W4_LOADS[i]
-            nc.sync.dma_start(out=w4_sb[i][:].bitcast(I32), in_=w4_i[:, a : a + n, first // 2 : (first + width) // 2])
+        def load_w4(a):
+            nc.sync.dma_start(out=w4_sb[a][:].bitcast(I32), in_=w4_i[a])
 
-        def load_up(i):
-            first, width = UP_LOADS[i]
-            if JSPLIT:
-                half = min(i, 1)
-                nc.sync.dma_start(out=u_raw[i][:], in_=up_v[:, 2 * half : 2 * half + 2, first : first + width])
-            else:
-                nc.sync.dma_start(out=u_raw[i][:], in_=up_v[:, :, first : first + width])
+        def load_up(g):
+            first, width = GROUPS[g]
+            nc.sync.dma_start(out=u_raw[g][:], in_=up_v[:, :, first : first + width])
 
-        def load_tab_scales(queue):
-            if MODE == "one":
-                queues[queue].dma_start(out=tab_rows[0:96:2, :], in_=tab_s)
-                return
-            if MODE == "direct":
-                rows = tab_i[:, WORD_COLS:].rearrange("a (q r t) -> r q a t", q=4, r=4)
-                for r in range(4):
-                    queues[queue].dma_start(
-                        out=tab_rows[r:P:32, :].rearrange("q (a t) -> q a t", a=PASSES), in_=rows[r]
-                    )
-                return
-            queues[queue].dma_start(out=tab_rows[ROW0 : ROW0 + 16 * STEP - STEP + 1 : STEP, :].rearrange("q (a t) -> q a t", a=PASSES), in_=tab_s)
-
-        def gather_scales():
+        def stage_scales():
+            nc.sync.dma_start(
+                out=tab_rows[STAGED, :].rearrange("q (a c) -> q a c", a=PASSES),
+                in_=tab_i[:, WORD_COLS:].rearrange("a (q c) -> q a c", q=BLOCKS),
+            )
+            nc.sync.dma_start(
+                out=stage[STAGED, :W4_COLS].rearrange("q (a c) -> q a c", a=PASSES),
+                in_=w4_scales.bitcast(I32).rearrange("a q c -> q a c"),
+            )
             tab_bytes = tab_rows[:].bitcast(U8)
-            for a in range(1 if MODE == "one" else PASSES):
+            for a in range(PASSES):
                 nc.vector.tensor_copy(
                     picked_rows[:, S * a : S * (a + 1)], tab_bytes[:, T * a : T * (a + 1)].indirect(offsets[:])
                 )
-            if MERGED:
-                nc.vector.tensor_copy(out=stage[:, W4_COLS:], in_=picked_rows[:].bitcast(I32))
+            nc.vector.tensor_copy(out=stage[:, W4_COLS:], in_=picked_rows[:].bitcast(I32))
 
-        def load_w4_scales(queue):
-            if MERGED:
-                w4_s = w4_scales.bitcast(I32).rearrange("a q n -> q a n")
-                queues[queue].dma_start(out=stage[ROW0 : ROW0 + 16 * STEP - STEP + 1 : STEP, :W4_COLS].rearrange("q (a n) -> q a n", a=PASSES), in_=w4_s)
-            else:
-                w4_s = w4_scales.bitcast(I32).rearrange("a (q r) n -> r q a n", q=4, r=4)
-                for r in range(4):
-                    queues[queue].dma_start(
-                        out=w4_plane[r:P:32, :].rearrange("q (a t) -> q a t", a=PASSES), in_=w4_s[r]
-                    )
-
-        def move_scales(queue):
-            for r in range(4):
-                if MODE == "one":
-                    queues[queue].dma_start(
-                        out=v_plane[32 * r : 32 * r + 4, :], in_=picked_rows[24 * r : 24 * (r + 1) : 2, :].bitcast(I32)
-                    )
-                elif MERGED:
-                    queues[queue].dma_start(out=plane[r:P:32, :], in_=stage[ROW0 + STEP * r : ROW0 + STEP * (r + 12) + 1 : 4 * STEP, :])
-                else:
-                    queues[queue].dma_start(out=v_plane[r:P:32, :], in_=picked_rows[ROW0 + STEP * r : ROW0 + STEP * (r + 12) + 1 : 4 * STEP, :].bitcast(I32))
-
-        w4_bytes = w4_plane.bitcast(U8)
-        if MODE == "direct":
-            v_plane = picked_rows[:].bitcast(I32)
-        v_scales = [v_plane.bitcast(U8)[:, S * a : S * (a + 1)] for a in range(PASSES)]
-        windows = [words[i][:, b, :] for i, (a, n) in enumerate(WORD_LOADS) for b in range(n)]
+        def carry_scales():
+            for i in range(4):
+                rows = slice(ROW0 + STEP * i, ROW0 + STEP * (i + 12) + 1, 4 * STEP)
+                nc.sync.dma_start(out=plane[i:P:32, :], in_=stage[rows, :])
 
         def gather_words(a):
-            nc.vector.tensor_copy(v_codes[a][:], windows[a].bitcast(U32).indirect(offsets[:]))
+            nc.vector.tensor_copy(v_codes[a][:], words[a][:].bitcast(U32).indirect(offsets[:]))
 
-        def group_down(a, split):
-            src = d_raw[a][:].rearrange("p j (m u e) -> p u m j e", u=2, e=2)
-            dst = d_grp[a][:].rearrange("p (u e) m j -> p u m j e", e=2)
-            if split > 0:
-                nc.vector.tensor_copy(out=dst[:, :, :split], in_=src[:, :, :split])
-            if split < P:
-                nc.scalar.copy(out=dst[:, :, split:], in_=src[:, :, split:])
+        def round_down(a):
+            share = DOWN_ON_VECTOR[a]
+            src = d_raw[a][:].rearrange("p t (m u e) -> p u m t e", u=2, e=2)
+            dst = d_grp[a][:].rearrange("p (u e) m t -> p u m t e", e=2)
+            if share > 0:
+                nc.vector.tensor_copy(out=dst[:, :, :share], in_=src[:, :, :share])
+            nc.scalar.copy(out=dst[:, :, share:], in_=src[:, :, share:])
 
         def quantize_down(a):
             nc.vector.quantize_mx(
                 out=d_codes[a][:].bitcast(FP8X4),
                 scales=d_scales[a][:],
-                in_=d_grp[a][:].rearrange("p t m j -> p (t m j)"),
+                in_=d_grp[a][:].rearrange("p s m t -> p (s m t)"),
             )
 
-        def group_up(c, on_vector, half=1):
+        def round_up(c):
             g, first, width = CHUNKS[c]
-            first += GROUPS[g][0]
-            if JSPLIT:
-                i = half * max(i for i, (f, w) in enumerate(UP_LOADS) if f <= first)
-                first -= UP_LOADS[i][0]
-                src = u_raw[i][:, :, first : first + width].rearrange("p j (c i) -> p c j i", i=4)
-                dst = u_grp[c][:, :, 2 * half : 2 * half + 2].rearrange("p (c i) j -> p c j i", i=4)
-                split = on_vector // 4
-                if split > 0:
-                    nc.vector.tensor_copy(out=dst[:, :split], in_=src[:, :split])
-                if on_vector < width:
-                    nc.scalar.copy(out=dst[:, split:], in_=src[:, split:])
-                return
-            i = max(i for i, (f, w) in enumerate(UP_LOADS) if f <= first)
-            first -= UP_LOADS[i][0]
-            src = u_raw[i][:, :, first : first + width].rearrange("p j (c i) -> p c j i", i=4)
-            dst = u_grp[c][:].rearrange("p (c i) j -> p c j i", i=4)
-            split = on_vector // 4
-            if split > 0:
-                nc.vector.tensor_copy(out=dst[:, :split], in_=src[:, :split])
-            if on_vector < width:
-                nc.scalar.copy(out=dst[:, split:], in_=src[:, split:])
+            share = UP_ON_VECTOR[c] // 4
+            src = u_raw[g][:, :, first : first + width].rearrange("p t (b i) -> p b t i", i=4)
+            dst = u_grp[c][:].rearrange("p (b i) t -> p b t i", i=4)
+            nc.vector.tensor_copy(out=dst[:, :share], in_=src[:, :share])
+            if UP_ON_VECTOR[c] < width:
+                nc.scalar.copy(out=dst[:, share:], in_=src[:, share:])
 
         def quantize_up(c):
             nc.vector.quantize_mx(
-                out=u_codes[c][:].bitcast(FP8X4), scales=u_scales[c][:], in_=u_grp[c][:].rearrange("p w j -> p (w j)")
+                out=u_codes[c][:].bitcast(FP8X4), scales=u_scales[c][:], in_=u_grp[c][:].rearrange("p n t -> p (n t)")
             )
 
-        def base(a, g, last=0):
-            first, width = GROUPS[g]
-            step = 512 if width == 512 else P
+        def multiply_down(a):
             for j in range(2):
                 js = slice(P * j, P * (j + 1))
-                for c in range(0, width, step):
-                    i = [i for i, (b, n, f, w) in enumerate(W4_LOADS) if b <= a < b + n and f <= first + c < f + w][0]
-                    inside = first + c - W4_LOADS[i][2]
+                for s in range(4):
+                    ss = slice(P * s, P * (s + 1))
                     nc.tensor.matmul_mx(
-                        out=o_ps[g][j][:, c : c + step],
-                        lhsT=v_codes[a][:, js].bitcast(FP8X4),
-                        lhsT_scale=v_scales[a][:, js],
-                        rhs=w4_sb[i][:, a - W4_LOADS[i][0], 2 * inside : 2 * (inside + step)].bitcast(FP4X4),
-                        rhs_scale=w4_bytes[:, a * M + first + c : a * M + first + c + step],
-                        start=(a == 0 and c == 0 and (j == 0 or g in SPLIT_BANKS)),
-                        stop=(last == 1 and c + step == width and (j == 1 or g in SPLIT_BANKS)),
-                    )
-
-        def low_rank(a):
-            for j in range(2):
-                js = slice(P * j, P * (j + 1))
-                for t in range(4):
-                    ts = slice(P * t, P * (t + 1))
-                    nc.tensor.matmul_mx(
-                        out=h_ps[j][:, t, :],
-                        lhsT=d_codes[a][:, ts].bitcast(FP8X4),
-                        lhsT_scale=d_scales[a][:, ts],
+                        out=h_ps[j][:, s, :],
+                        lhsT=d_codes[a][:, ss].bitcast(FP8X4),
+                        lhsT_scale=d_scales[a][:, ss],
                         rhs=v_codes[a][:, js].bitcast(FP8X4),
-                        rhs_scale=v_scales[a][:, js],
-                        start=(a == 0 and t == 0),
-                        stop=(a == PASSES - 1 and t == 3),
+                        rhs_scale=v_planes[a][:, js],
+                        start=(a == 0 and s == 0),
+                        stop=(a == PASSES - 1 and s == 3),
                     )
 
-        def move(dst, src, on_vector):
-            if on_vector:
-                nc.vector.tensor_copy(out=dst, in_=src)
-            else:
-                nc.scalar.copy(out=dst, in_=src)
+        def quantize_h():
+            nc.scalar.copy(out=h_grp[0][:], in_=h_ps[0][:].rearrange("p s n -> p n s"))
+            nc.vector.tensor_copy(out=h_grp[1][:], in_=h_ps[1][:].rearrange("p s n -> p n s"))
+            for j in range(2):
+                nc.vector.quantize_mx(
+                    out=h_codes[j][:].bitcast(FP8X4),
+                    scales=h_scales[j][:],
+                    in_=h_grp[j][:].rearrange("p n s -> p (n s)"),
+                )
 
-        def group_h(j, on_vector):
-            move(h_grp[j][:], h_ps[j][:].rearrange("p t n -> p n t"), on_vector)
+        def multiply_w4(a, g):
+            first, width = GROUPS[g]
+            step = BANK if width == BANK else P
+            for j in range(2):
+                js = slice(P * j, P * (j + 1))
+                for n in range(0, width, step):
+                    col = first + n
+                    nc.tensor.matmul_mx(
+                        out=o_ps[g][j][:, n : n + step],
+                        lhsT=v_codes[a][:, js].bitcast(FP8X4),
+                        lhsT_scale=v_planes[a][:, js],
+                        rhs=w4_sb[a][:, 2 * col : 2 * (col + step)].bitcast(FP4X4),
+                        rhs_scale=w4_plane[:, a * M + col : a * M + col + step],
+                        start=(a == 0 and n == 0),
+                        stop=False,
+                    )
 
-        def quantize_h(j):
-            nc.vector.quantize_mx(
-                out=h_codes[j][:].bitcast(FP8X4), scales=h_scales[j][:], in_=h_grp[j][:].rearrange("p w j -> p (w j)")
-            )
-
-        def close(c, may_stop=1):
+        def multiply_up(c):
             g, first, width = CHUNKS[c]
             for j in range(2):
                 nc.tensor.matmul_mx(
@@ -274,26 +192,76 @@ def tile_list_tablora_tm_none_kernel(tc, tab, w4_words, w4_scales, down, up, off
                     rhs=u_codes[c][:].bitcast(FP8X4),
                     rhs_scale=u_scales[c][:],
                     start=False,
-                    stop=(may_stop == 1 and first + width == GROUPS[g][1] and (j == 1 or g in SPLIT_BANKS)),
+                    stop=(first + width == GROUPS[g][1]),
                 )
 
-        def store(g, on_vector, apart):
+        def store(g, j, queue=nc.sync):
             first, width = GROUPS[g]
-            if g in SPLIT_BANKS:
-                for j in range(2):
-                    move(o_sb[g][:, j, :], o_ps[g][j], j in on_vector)
-                    if apart:
-                        nc.sync.dma_start(out=out_v[:, j, first : first + width], in_=o_sb[g][:, j, :])
-            else:
-                move(o_sb[g][:], o_ps[g][2], 0 in on_vector)
-            if not apart:
-                nc.sync.dma_start(out=out_v[:, :, first : first + width], in_=o_sb[g][:])
+            queue.dma_start(out=out_v[:, j, first : first + width], in_=o_sb[g][:, j, :])
 
-        calls = {
-            "list": load_list, "down": load_down, "words": load_words, "w4": load_w4, "up": load_up,
-            "ts": load_tab_scales, "gs": gather_scales, "ws": load_w4_scales, "mv": move_scales,
-            "ga": lambda c, on_vector: group_up(c, on_vector, 0), "gw": gather_words, "gd": group_down, "qd": quantize_down, "gu": group_up, "qu": quantize_up,
-            "base": base, "lr": low_rank, "gh": group_h, "qh": quantize_h, "close": close, "store": store,
-        }
-        for step in LOADS + STEPS:
-            calls[step[0]](*step[1:])
+        nc.vector.memset(tab_rows[:], 0)
+        nc.vector.memset(plane[:], 0)
+
+        load_down(0)
+        nc.sync.dma_start(offsets[:], offs)
+        stage_scales()
+        load_down(1)
+        load_words(0)
+        load_down(2)
+        carry_scales()
+        load_words(1)
+        load_words(2)
+        load_w4(0)
+        load_up(0)
+        load_w4(1)
+        load_w4(2)
+        load_up(1)
+        load_up(2)
+
+        round_down(0)
+        quantize_down(0)
+        gather_words(0)
+        round_down(1)
+        quantize_down(1)
+        multiply_down(0)
+        round_down(2)
+        quantize_down(2)
+        for a in range(1, PASSES):
+            gather_words(a)
+            multiply_down(a)
+        quantize_h()
+
+        for g in range(len(GROUPS)):
+            multiply_w4(0, g)
+        round_up(0)
+        round_up(1)
+        for a in range(1, PASSES):
+            multiply_w4(a, 0)
+        for c in range(2):
+            quantize_up(c)
+            multiply_up(c)
+        for j in range(2):
+            nc.scalar.copy(out=o_sb[0][:, j, :], in_=o_ps[0][j][:])
+            store(0, j)
+
+        for a in range(1, PASSES):
+            multiply_w4(a, 1)
+        round_up(2)
+        quantize_up(2)
+        multiply_up(2)
+
+        for a in range(1, PASSES):
+            multiply_w4(a, 2)
+        round_up(3)
+        round_up(4)
+        quantize_up(3)
+        multiply_up(3)
+        quantize_up(4)
+        for j in range(2):
+            nc.scalar.copy(out=o_sb[1][:, j, :], in_=o_ps[1][j][:])
+        nc.scalar.dma_start(out=out_v[:, :, GROUPS[1][0] : GROUPS[2][0]], in_=o_sb[1][:])
+        multiply_up(4)
+        nc.scalar.copy(out=o_sb[2][:, 0, :], in_=o_ps[2][0][:])
+        store(2, 0, nc.scalar)
+        nc.vector.tensor_copy(out=o_sb[2][:, 1, :], in_=o_ps[2][1][:])
+        store(2, 1)

@@ -25,9 +25,12 @@ V_COLS = PASSES * S // 4
 ROW0, STEP = 32, 4
 STAGED = slice(ROW0, ROW0 + STEP * (BLOCKS - 1) + 1, STEP)
 
-GROUPS = ((0, 512), (512, 256), (768, 256))
-CHUNKS = ((0, 0, 256), (0, 256, 256), (1, 0, 256), (2, 0, 128), (2, 128, 128))
-UP_ON_VECTOR = (160, 160, 256, 80, 96)
+PIECES = ((0, 512), (512, 256), (768, 256))
+CHUNKS = ((0, 256, 160), (256, 256, 160), (512, 256, 256), (768, 128, 80), (896, 128, 96))
+SUMS = ((0, 512, ('a', 'b')), (512, 256, ('c', 'd')), (768, 128, ('e', 'f')), (896, 128, ('h0', 'h1')))
+STORES = ((0, 512), (512, 256), (768, 256))
+W4LOADS = ((0, 1, 0, 1024), (1, 2, 0, 1024), (2, 3, 0, 1024))
+WORDLOADS = ((0, 1), (1, 2), (2, 3))
 DOWN_ON_VECTOR = (0, 0, 88)
 
 
@@ -41,29 +44,36 @@ def tile_list_tablora_tm_none_kernel(tc, tab, w4_words, w4_scales, down, up, off
             return keep.tile(shape, dtype, name=name, align_bytes=64)
 
         offsets = keep.tile([P, S // 16], U16, name="offsets")
-        words = [sbuf(f"words{a}", [P, T], I32) for a in range(PASSES)]
+        words = [sbuf(f"words{i}", [P, (a1 - a0) * T], I32) for i, (a0, a1) in enumerate(WORDLOADS)]
         tab_rows = sbuf("tab_rows", [P, PASSES * T // 4], I32)
         picked_rows = sbuf("picked_rows", [P, PASSES * S], U8)
         stage = sbuf("stage", [P, W4_COLS + V_COLS], I32)
         plane = sbuf("plane", [P, W4_COLS + V_COLS], I32)
-        w4_sb = [sbuf(f"w4_sb{a}", [P, 2 * M], U8) for a in range(PASSES)]
+        w4_sb = [sbuf(f"w4_sb{i}", [P, (a1 - a0) * 2 * width], U8) for i, (a0, a1, first, width) in enumerate(W4LOADS)]
         d_raw = [sbuf(f"d_raw{a}", [P, 4, R], F32) for a in range(PASSES)]
         d_grp = [sbuf(f"d_grp{a}", [P, 4, P, 4], BF16) for a in range(PASSES)]
         d_codes = [sbuf(f"d_codes{a}", [P, R], U32) for a in range(PASSES)]
         d_scales = [sbuf(f"d_scales{a}", [P, R], U8) for a in range(PASSES)]
-        u_raw = [sbuf(f"u_raw{g}", [P, 4, width], F32) for g, (first, width) in enumerate(GROUPS)]
-        u_grp = [sbuf(f"u_grp{c}", [P, width, 4], BF16) for c, (g, first, width) in enumerate(CHUNKS)]
-        u_codes = [sbuf(f"u_codes{c}", [P, width], U32) for c, (g, first, width) in enumerate(CHUNKS)]
-        u_scales = [sbuf(f"u_scales{c}", [P, width], U8) for c, (g, first, width) in enumerate(CHUNKS)]
+        u_raw = [sbuf(f"u_raw{g}", [P, 4, width], F32) for g, (first, width) in enumerate(PIECES)]
+        u_grp = [sbuf(f"u_grp{c}", [P, width, 4], BF16) for c, (first, width, share) in enumerate(CHUNKS)]
+        u_codes = [sbuf(f"u_codes{c}", [P, width], U32) for c, (first, width, share) in enumerate(CHUNKS)]
+        u_scales = [sbuf(f"u_scales{c}", [P, width], U8) for c, (first, width, share) in enumerate(CHUNKS)]
         v_codes = [sbuf(f"v_codes{a}", [P, S], U32) for a in range(PASSES)]
         h_grp = [sbuf(f"h_grp{j}", [P, P, 4], BF16) for j in range(2)]
         h_codes = [sbuf(f"h_codes{j}", [P, P], U32) for j in range(2)]
         h_scales = [sbuf(f"h_scales{j}", [P, P], U8) for j in range(2)]
-        o_sb = [sbuf(f"o_sb{g}", [P, 2, width], F32) for g, (first, width) in enumerate(GROUPS)]
-        h_ps = [psum.tile([P, 4, P], F32, name=f"h_ps{j}") for j in range(2)]
-        o_ps = [
-            [psum.tile([P, width], F32, name=f"o_ps{g}{j}") for j in range(2)] for g, (first, width) in enumerate(GROUPS)
-        ]
+        o_sb = [sbuf(f"o_sb{g}", [P, 2, width], F32) for g, (first, width) in enumerate(STORES)]
+        h_ps = [psum.tile([P, 4, P], F32, name=f"h_ps{j}", tag=f"h{j}") for j in range(2)]
+        o_ps = {}
+        opened = set()
+
+        def bank(g, j):
+            first, width, tags = SUMS[g]
+            tag = tags[j % len(tags)]
+            if tag not in o_ps:
+                o_ps[tag] = psum.tile([P, 2 * width // len(tags)], F32, name=f"o_ps{g}{j}", tag=tag)
+            at = 0 if len(tags) == 2 else j * width
+            return tag, o_ps[tag][:, at : at + width]
 
         tab_i = tab.bitcast(I32)
         w4_i = w4_words.bitcast(I32)
@@ -77,14 +87,22 @@ def tile_list_tablora_tm_none_kernel(tc, tab, w4_words, w4_scales, down, up, off
                 out=d_raw[a][:], in_=down[512 * a : 512 * (a + 1), :].rearrange("(p t) r -> p t r", t=4)
             )
 
-        def load_words(a):
-            nc.sync.dma_start(out=words[a][:], in_=tab_i[a, :WORD_COLS].rearrange("(p c) -> p c", p=P))
+        def load_words(i):
+            a0, a1 = WORDLOADS[i]
+            nc.sync.dma_start(
+                out=words[i][:].rearrange("p (a c) -> p a c", c=T),
+                in_=tab_i[a0:a1, :WORD_COLS].rearrange("a (p c) -> p a c", p=P),
+            )
 
-        def load_w4(a):
-            nc.sync.dma_start(out=w4_sb[a][:].bitcast(I32), in_=w4_i[a])
+        def load_w4(i):
+            a0, a1, first, width = W4LOADS[i]
+            nc.sync.dma_start(
+                out=w4_sb[i][:].bitcast(I32).rearrange("p (a c) -> p a c", a=a1 - a0),
+                in_=w4_i[a0:a1, :, first // 2 : (first + width) // 2].rearrange("a p c -> p a c"),
+            )
 
         def load_up(g):
-            first, width = GROUPS[g]
+            first, width = PIECES[g]
             nc.sync.dma_start(out=u_raw[g][:], in_=up_v[:, :, first : first + width])
 
         def stage_scales():
@@ -109,7 +127,9 @@ def tile_list_tablora_tm_none_kernel(tc, tab, w4_words, w4_scales, down, up, off
                 nc.sync.dma_start(out=plane[i:P:32, :], in_=stage[rows, :])
 
         def gather_words(a):
-            nc.vector.tensor_copy(v_codes[a][:], words[a][:].bitcast(U32).indirect(offsets[:]))
+            i = [k for k, (a0, a1) in enumerate(WORDLOADS) if a0 <= a < a1][0]
+            at = (a - WORDLOADS[i][0]) * T
+            nc.vector.tensor_copy(v_codes[a][:], words[i][:, at : at + T].bitcast(U32).indirect(offsets[:]))
 
         def round_down(a):
             share = DOWN_ON_VECTOR[a]
@@ -126,14 +146,16 @@ def tile_list_tablora_tm_none_kernel(tc, tab, w4_words, w4_scales, down, up, off
                 in_=d_grp[a][:].rearrange("p s m t -> p (s m t)"),
             )
 
-        def round_up(c):
-            g, first, width = CHUNKS[c]
-            share = UP_ON_VECTOR[c] // 4
-            src = u_raw[g][:, :, first : first + width].rearrange("p t (b i) -> p b t i", i=4)
+        def round_up(c, engines="vs"):
+            first, width, share = CHUNKS[c]
+            g = [k for k, (f, w) in enumerate(PIECES) if f <= first < f + w][0]
+            at = first - PIECES[g][0]
+            src = u_raw[g][:, :, at : at + width].rearrange("p t (b i) -> p b t i", i=4)
             dst = u_grp[c][:].rearrange("p (b i) t -> p b t i", i=4)
-            nc.vector.tensor_copy(out=dst[:, :share], in_=src[:, :share])
-            if UP_ON_VECTOR[c] < width:
-                nc.scalar.copy(out=dst[:, share:], in_=src[:, share:])
+            if share > 0 and "v" in engines:
+                nc.vector.tensor_copy(out=dst[:, : share // 4], in_=src[:, : share // 4])
+            if share < width and "s" in engines:
+                nc.scalar.copy(out=dst[:, share // 4 :], in_=src[:, share // 4 :])
 
         def quantize_up(c):
             nc.vector.quantize_mx(
@@ -155,49 +177,78 @@ def tile_list_tablora_tm_none_kernel(tc, tab, w4_words, w4_scales, down, up, off
                         stop=(a == PASSES - 1 and s == 3),
                     )
 
-        def quantize_h():
-            nc.scalar.copy(out=h_grp[0][:], in_=h_ps[0][:].rearrange("p s n -> p n s"))
-            nc.vector.tensor_copy(out=h_grp[1][:], in_=h_ps[1][:].rearrange("p s n -> p n s"))
-            for j in range(2):
-                nc.vector.quantize_mx(
-                    out=h_codes[j][:].bitcast(FP8X4),
-                    scales=h_scales[j][:],
-                    in_=h_grp[j][:].rearrange("p n s -> p (n s)"),
-                )
+        def empty_h(j, engine):
+            if engine == "s":
+                nc.scalar.copy(out=h_grp[j][:], in_=h_ps[j][:].rearrange("p s n -> p n s"))
+            else:
+                nc.vector.tensor_copy(out=h_grp[j][:], in_=h_ps[j][:].rearrange("p s n -> p n s"))
 
-        def multiply_w4(a, g):
-            first, width = GROUPS[g]
+        def quantize_h(j):
+            nc.vector.quantize_mx(
+                out=h_codes[j][:].bitcast(FP8X4),
+                scales=h_scales[j][:],
+                in_=h_grp[j][:].rearrange("p n s -> p (n s)"),
+            )
+
+        def multiply_w4(a, g, halves=(0, 1), stop=False):
+            first, width, tags = SUMS[g]
             step = BANK if width == BANK else P
-            for j in range(2):
+            for j in halves:
                 js = slice(P * j, P * (j + 1))
+                tag, acc = bank(g, j)
                 for n in range(0, width, step):
                     col = first + n
+                    i = [k for k, (a0, a1, f, w) in enumerate(W4LOADS) if a0 <= a < a1 and f <= col < f + w][0]
+                    a0, a1, f, w = W4LOADS[i]
+                    at = (a - a0) * w + col - f
                     nc.tensor.matmul_mx(
-                        out=o_ps[g][j][:, n : n + step],
+                        out=acc[:, n : n + step],
                         lhsT=v_codes[a][:, js].bitcast(FP8X4),
                         lhsT_scale=v_planes[a][:, js],
-                        rhs=w4_sb[a][:, 2 * col : 2 * (col + step)].bitcast(FP4X4),
+                        rhs=w4_sb[i][:, 2 * at : 2 * (at + step)].bitcast(FP4X4),
                         rhs_scale=w4_plane[:, a * M + col : a * M + col + step],
-                        start=(a == 0 and n == 0),
-                        stop=False,
+                        start=tag not in opened,
+                        stop=stop and n + step == width and (len(tags) == 2 or j == 1),
                     )
+                    opened.add(tag)
 
-        def multiply_up(c):
-            g, first, width = CHUNKS[c]
-            for j in range(2):
+        def multiply_up(c, halves=(0, 1), stop=False):
+            first, width, share = CHUNKS[c]
+            g = [k for k, (f, w, tags) in enumerate(SUMS) if f <= first < f + w][0]
+            at = first - SUMS[g][0]
+            for j in halves:
+                tag, acc = bank(g, j)
                 nc.tensor.matmul_mx(
-                    out=o_ps[g][j][:, first : first + width],
+                    out=acc[:, at : at + width],
                     lhsT=h_codes[j][:].bitcast(FP8X4),
                     lhsT_scale=h_scales[j][:],
                     rhs=u_codes[c][:].bitcast(FP8X4),
                     rhs_scale=u_scales[c][:],
-                    start=False,
-                    stop=(first + width == GROUPS[g][1]),
+                    start=tag not in opened,
+                    stop=stop and (len(SUMS[g][2]) == 2 or j == 1),
                 )
+                opened.add(tag)
 
-        def store(g, j, queue=nc.sync):
-            first, width = GROUPS[g]
-            queue.dma_start(out=out_v[:, j, first : first + width], in_=o_sb[g][:, j, :])
+        def empty(g, j, engine):
+            first, width, tags = SUMS[g]
+            k = [k for k, (f, w) in enumerate(STORES) if f <= first < f + w][0]
+            at = first - STORES[k][0]
+            if len(tags) == 2:
+                dst, src = o_sb[k][:, j, at : at + width], bank(g, j)[1]
+            else:
+                dst, src = o_sb[k][:, :, at : at + width], o_ps[tags[0]][:].rearrange("p (j n) -> p j n", j=2)
+            if engine == "s":
+                nc.scalar.copy(out=dst, in_=src)
+            else:
+                nc.vector.tensor_copy(out=dst, in_=src)
+
+        def store(k, j, engine):
+            first, width = STORES[k]
+            queue = nc.scalar if engine == "s" else nc.sync
+            if j < 2:
+                queue.dma_start(out=out_v[:, j, first : first + width], in_=o_sb[k][:, j, :])
+            else:
+                queue.dma_start(out=out_v[:, :, first : first + width], in_=o_sb[k][:])
 
         nc.vector.memset(tab_rows[:], 0)
         nc.vector.memset(plane[:], 0)
@@ -217,7 +268,6 @@ def tile_list_tablora_tm_none_kernel(tc, tab, w4_words, w4_scales, down, up, off
         load_w4(2)
         load_up(1)
         load_up(2)
-
         round_down(0)
         quantize_down(0)
         gather_words(0)
@@ -226,42 +276,54 @@ def tile_list_tablora_tm_none_kernel(tc, tab, w4_words, w4_scales, down, up, off
         multiply_down(0)
         round_down(2)
         quantize_down(2)
-        for a in range(1, PASSES):
-            gather_words(a)
-            multiply_down(a)
-        quantize_h()
-
-        for g in range(len(GROUPS)):
-            multiply_w4(0, g)
+        gather_words(1)
+        multiply_down(1)
+        gather_words(2)
+        multiply_down(2)
+        empty_h(0, "s")
+        empty_h(1, "v")
+        quantize_h(0)
+        quantize_h(1)
+        multiply_w4(0, 0)
+        multiply_w4(0, 1)
+        multiply_w4(0, 2)
+        multiply_w4(0, 3)
         round_up(0)
         round_up(1)
-        for a in range(1, PASSES):
-            multiply_w4(a, 0)
-        for c in range(2):
-            quantize_up(c)
-            multiply_up(c)
-        for j in range(2):
-            nc.scalar.copy(out=o_sb[0][:, j, :], in_=o_ps[0][j][:])
-            store(0, j)
-
-        for a in range(1, PASSES):
-            multiply_w4(a, 1)
+        multiply_w4(1, 0)
+        quantize_up(0)
+        quantize_up(1)
+        multiply_w4(2, 0, (0,))
+        multiply_up(0, (0,))
+        multiply_up(1, (0,), stop=True)
+        multiply_w4(2, 0, (1,))
+        multiply_up(0, (1,))
+        multiply_up(1, (1,), stop=True)
+        empty(0, 0, "s")
+        store(0, 0, "y")
+        empty(0, 1, "s")
+        store(0, 1, "y")
+        multiply_w4(1, 1)
+        multiply_w4(2, 1)
         round_up(2)
         quantize_up(2)
-        multiply_up(2)
-
-        for a in range(1, PASSES):
-            multiply_w4(a, 2)
+        multiply_up(2, stop=True)
+        multiply_w4(1, 2)
+        multiply_w4(2, 2)
+        multiply_w4(1, 3)
+        multiply_w4(2, 3)
         round_up(3)
         round_up(4)
         quantize_up(3)
-        multiply_up(3)
+        multiply_up(3, stop=True)
         quantize_up(4)
-        for j in range(2):
-            nc.scalar.copy(out=o_sb[1][:, j, :], in_=o_ps[1][j][:])
-        nc.scalar.dma_start(out=out_v[:, :, GROUPS[1][0] : GROUPS[2][0]], in_=o_sb[1][:])
-        multiply_up(4)
-        nc.scalar.copy(out=o_sb[2][:, 0, :], in_=o_ps[2][0][:])
-        store(2, 0, nc.scalar)
-        nc.vector.tensor_copy(out=o_sb[2][:, 1, :], in_=o_ps[2][1][:])
-        store(2, 1)
+        empty(1, 0, "s")
+        store(1, 0, "y")
+        empty(1, 1, "s")
+        store(1, 1, "y")
+        multiply_up(4, stop=True)
+        empty(2, 0, "s")
+        empty(2, 1, "v")
+        empty(3, 0, "s")
+        empty(3, 1, "v")
+        store(2, 2, "y")

@@ -325,5 +325,6 @@ def tile_list_tablora_tm_none_kernel(tc, tab, w4_words, w4_scales, down, up, off
         empty(2, 0, "s")
         empty(2, 1, "v")
         empty(3, 0, "s")
+        store(2, 0, "s")
         empty(3, 1, "v")
-        store(2, 2, "y")
+        store(2, 1, "y")

@@ -22,7 +22,7 @@ WORD_COLS = 512 * T // 4
 W4_COLS = PASSES * M // 4
 V_COLS = PASSES * S // 4
 
-ROW0, STEP = 32, 4
+ROW0, STEP = 0, 8
 STAGED = slice(ROW0, ROW0 + STEP * (BLOCKS - 1) + 1, STEP)
 
 PIECES = ((0, 512), (512, 256), (768, 256))
@@ -47,7 +47,6 @@ def tile_list_tablora_tm_none_kernel(tc, tab, w4_words, w4_scales, down, up, off
         words = [sbuf(f"words{i}", [P, (a1 - a0) * T], I32) for i, (a0, a1) in enumerate(WORDLOADS)]
         tab_rows = sbuf("tab_rows", [P, PASSES * T // 4], I32)
         picked_rows = sbuf("picked_rows", [P, PASSES * S], U8)
-        stage = sbuf("stage", [P, W4_COLS + V_COLS], I32)
         plane = sbuf("plane", [P, W4_COLS + V_COLS], I32)
         w4_sb = [sbuf(f"w4_sb{i}", [P, (a1 - a0) * 2 * width], U8) for i, (a0, a1, first, width) in enumerate(W4LOADS)]
         d_raw = [sbuf(f"d_raw{a}", [P, 4, R], F32) for a in range(PASSES)]
@@ -111,7 +110,7 @@ def tile_list_tablora_tm_none_kernel(tc, tab, w4_words, w4_scales, down, up, off
                 in_=tab_i[:, WORD_COLS:].rearrange("a (q c) -> q a c", q=BLOCKS),
             )
             nc.sync.dma_start(
-                out=stage[STAGED, :W4_COLS].rearrange("q (a c) -> q a c", a=PASSES),
+                out=plane[STAGED, :W4_COLS].rearrange("q (a c) -> q a c", a=PASSES),
                 in_=w4_scales.bitcast(I32).rearrange("a q c -> q a c"),
             )
             tab_bytes = tab_rows[:].bitcast(U8)
@@ -119,12 +118,12 @@ def tile_list_tablora_tm_none_kernel(tc, tab, w4_words, w4_scales, down, up, off
                 nc.vector.tensor_copy(
                     picked_rows[:, S * a : S * (a + 1)], tab_bytes[:, T * a : T * (a + 1)].indirect(offsets[:])
                 )
-            nc.vector.tensor_copy(out=stage[:, W4_COLS:], in_=picked_rows[:].bitcast(I32))
+            nc.vector.tensor_copy(out=plane[:, W4_COLS:], in_=picked_rows[:].bitcast(I32))
 
         def carry_scales():
-            for i in range(4):
+            for i in range(1, 4):
                 rows = slice(ROW0 + STEP * i, ROW0 + STEP * (i + 12) + 1, 4 * STEP)
-                nc.sync.dma_start(out=plane[i:P:32, :], in_=stage[rows, :])
+                nc.sync.dma_start(out=plane[i:P:32, :], in_=plane[rows, :])
 
         def gather_words(a):
             i = [k for k, (a0, a1) in enumerate(WORDLOADS) if a0 <= a < a1][0]
@@ -251,7 +250,7 @@ def tile_list_tablora_tm_none_kernel(tc, tab, w4_words, w4_scales, down, up, off
                 queue.dma_start(out=out_v[:, :, first : first + width], in_=o_sb[k][:])
 
         nc.vector.memset(tab_rows[:], 0)
-        nc.vector.memset(plane[:], 0)
+        nc.vector.memset(plane[:, :W4_COLS], 0)
 
         load_down(0)
         nc.sync.dma_start(offsets[:], offs)

@@ -324,6 +324,5 @@ def tile_list_tablora_tm_none_kernel(tc, tab, w4_words, w4_scales, down, up, off
         empty(2, 0, "s")
         empty(2, 1, "v")
         empty(3, 0, "s")
-        store(2, 0, "s")
         empty(3, 1, "v")
-        store(2, 1, "y")
+        store(2, 2, "y")

@@ -41,7 +41,7 @@ def tile_list_tablora_tm_none_kernel(tc, tab, w4_words, w4_scales, down, up, off
         psum = ctx.enter_context(tc.psum_pool(name="psum", bufs=1))
 
         def sbuf(name, shape, dtype):
-            return keep.tile(shape, dtype, name=name, align_bytes=64)
+            return keep.tile(shape, dtype, name=name, align_bytes=256)
 
         offsets = keep.tile([P, S // 16], U16, name="offsets")
         words = [sbuf(f"words{i}", [P, (a1 - a0) * T], I32) for i, (a0, a1) in enumerate(WORDLOADS)]

@@ -28,7 +28,7 @@ STAGED = slice(ROW0, ROW0 + STEP * (BLOCKS - 1) + 1, STEP)
 PIECES = ((0, 512), (512, 256), (768, 256))
 CHUNKS = ((0, 256, 160), (256, 256, 160), (512, 256, 256), (768, 128, 80), (896, 128, 96))
 SUMS = ((0, 512, ('a', 'b')), (512, 256, ('c', 'd')), (768, 128, ('e', 'f')), (896, 128, ('h0', 'h1')))
-STORES = ((0, 512), (512, 256), (768, 256))
+STORES = ((0, 512), (512, 256), (768, 128), (896, 128))
 W4LOADS = ((0, 1, 0, 1024), (1, 2, 0, 1024), (2, 3, 0, 1024))
 WORDLOADS = ((0, 1), (1, 2), (2, 3))
 DOWN_ON_VECTOR = (0, 0, 88)
@@ -41,7 +41,7 @@ def tile_list_tablora_tm_none_kernel(tc, tab, w4_words, w4_scales, down, up, off
         psum = ctx.enter_context(tc.psum_pool(name="psum", bufs=1))
 
         def sbuf(name, shape, dtype):
-            return keep.tile(shape, dtype, name=name, align_bytes=256)
+            return keep.tile(shape, dtype, name=name, align_bytes=1024)
 
         offsets = keep.tile([P, S // 16], U16, name="offsets")
         words = [sbuf(f"words{i}", [P, (a1 - a0) * T], I32) for i, (a0, a1) in enumerate(WORDLOADS)]
@@ -176,6 +176,19 @@ def tile_list_tablora_tm_none_kernel(tc, tab, w4_words, w4_scales, down, up, off
                         stop=(a == PASSES - 1 and s == 3),
                     )
 
+        def warm_tensor(a):
+            unread = psum.tile([P, BANK], F32, name="unread", tag="e")
+            for repeat in range(2):
+                nc.tensor.matmul_mx(
+                    out=unread[:],
+                    lhsT=d_codes[a][:, :P].bitcast(FP8X4),
+                    lhsT_scale=d_scales[a][:, :P],
+                    rhs=d_codes[a][:].bitcast(FP8X4),
+                    rhs_scale=d_scales[a][:],
+                    start=True,
+                    stop=True,
+                )
+
         def empty_h(j, engine):
             if engine == "s":
                 nc.scalar.copy(out=h_grp[j][:], in_=h_ps[j][:].rearrange("p s n -> p n s"))
@@ -272,6 +285,7 @@ def tile_list_tablora_tm_none_kernel(tc, tab, w4_words, w4_scales, down, up, off
         gather_words(0)
         round_down(1)
         quantize_down(1)
+        warm_tensor(1)
         multiply_down(0)
         round_down(2)
         quantize_down(2)
@@ -323,6 +337,7 @@ def tile_list_tablora_tm_none_kernel(tc, tab, w4_words, w4_scales, down, up, off
         multiply_up(4, stop=True)
         empty(2, 0, "s")
         empty(2, 1, "v")
+        store(2, 2, "y")
         empty(3, 0, "s")
         empty(3, 1, "v")
-        store(2, 2, "y")
+        store(3, 2, "y")

@@ -26,7 +26,7 @@ ROW0, STEP = 0, 8
 STAGED = slice(ROW0, ROW0 + STEP * (BLOCKS - 1) + 1, STEP)
 
 PIECES = ((0, 512), (512, 256), (768, 256))
-CHUNKS = ((0, 256, 160), (256, 256, 160), (512, 256, 256), (768, 128, 80), (896, 128, 96))
+CHUNKS = ((0, 256, 160), (256, 256, 160), (512, 256, 256), (768, 128, 80), (896, 128, 128))
 SUMS = ((0, 512, ('a', 'b')), (512, 256, ('c', 'd')), (768, 128, ('e', 'f')), (896, 128, ('h0', 'h1')))
 STORES = ((0, 512), (512, 256), (768, 128), (896, 128))
 W4LOADS = ((0, 1, 0, 1024), (1, 2, 0, 1024), (2, 3, 0, 1024))

@@ -26,10 +26,19 @@ ROW0, STEP = 0, 8
 STAGED = slice(ROW0, ROW0 + STEP * (BLOCKS - 1) + 1, STEP)
 
 PIECES = ((0, 512), (512, 256), (768, 256))
-CHUNKS = ((0, 256, 160), (256, 256, 160), (512, 256, 256), (768, 128, 80), (896, 128, 128))
-SUMS = ((0, 512, ('a', 'b')), (512, 256, ('c', 'd')), (768, 128, ('e', 'f')), (896, 128, ('h0', 'h1')))
+CHUNKS = ((0, 256, 160), (256, 256, 160), (512, 256, 256), (768, 128, 128), (896, 128, 128))
+BANKS = (
+    ("a", (0,), 0, 256),
+    ("b", (0,), 256, 256),
+    ("c", (1,), 0, 512),
+    ("d", (0, 1), 512, 256),
+    ("e", (0,), 768, 128),
+    ("f", (1,), 768, 128),
+    ("h0", (0,), 896, 128),
+    ("h1", (1,), 896, 128),
+)
 STORES = ((0, 512), (512, 256), (768, 128), (896, 128))
-W4LOADS = ((0, 1, 0, 1024), (1, 2, 0, 1024), (2, 3, 0, 1024))
+W4LOADS = (((0, 0), (1, 0)), ((1, 1), (2, 0)), ((0, 1), (2, 1)))
 WORDLOADS = ((0, 1), (1, 2), (2, 3))
 DOWN_ON_VECTOR = (0, 0, 88)
 
@@ -48,7 +57,7 @@ def tile_list_tablora_tm_none_kernel(tc, tab, w4_words, w4_scales, down, up, off
         tab_rows = sbuf("tab_rows", [P, PASSES * T // 4], I32)
         picked_rows = sbuf("picked_rows", [P, PASSES * S], U8)
         plane = sbuf("plane", [P, W4_COLS + V_COLS], I32)
-        w4_sb = [sbuf(f"w4_sb{i}", [P, (a1 - a0) * 2 * width], U8) for i, (a0, a1, first, width) in enumerate(W4LOADS)]
+        w4_sb = [sbuf(f"w4_sb{i}", [P, 2 * M], U8) for i in range(len(W4LOADS))]
         d_raw = [sbuf(f"d_raw{a}", [P, 4, R], F32) for a in range(PASSES)]
         d_grp = [sbuf(f"d_grp{a}", [P, 4, P, 4], BF16) for a in range(PASSES)]
         d_codes = [sbuf(f"d_codes{a}", [P, R], U32) for a in range(PASSES)]
@@ -64,15 +73,24 @@ def tile_list_tablora_tm_none_kernel(tc, tab, w4_words, w4_scales, down, up, off
         o_sb = [sbuf(f"o_sb{g}", [P, 2, width], F32) for g, (first, width) in enumerate(STORES)]
         h_ps = [psum.tile([P, 4, P], F32, name=f"h_ps{j}", tag=f"h{j}") for j in range(2)]
         o_ps = {}
-        opened = set()
+        summed = {}
 
-        def bank(g, j):
-            first, width, tags = SUMS[g]
-            tag = tags[j % len(tags)]
-            if tag not in o_ps:
-                o_ps[tag] = psum.tile([P, 2 * width // len(tags)], F32, name=f"o_ps{g}{j}", tag=tag)
-            at = 0 if len(tags) == 2 else j * width
-            return tag, o_ps[tag][:, at : at + width]
+        def accumulate(b, j, col, n, lhsT, lhsT_scale, rhs, rhs_scale):
+            tag, halves, first, width = BANKS[b]
+            if b not in o_ps:
+                o_ps[b] = psum.tile([P, len(halves), width], F32, name=f"o_ps{b}", tag=tag)
+                summed[b] = 0
+            start = summed[b] == 0
+            summed[b] = summed[b] + n
+            nc.tensor.matmul_mx(
+                out=o_ps[b][:, halves.index(j), col - first : col - first + n],
+                lhsT=lhsT,
+                lhsT_scale=lhsT_scale,
+                rhs=rhs,
+                rhs_scale=rhs_scale,
+                start=start,
+                stop=summed[b] == (PASSES + 1) * len(halves) * width,
+            )
 
         tab_i = tab.bitcast(I32)
         w4_i = w4_words.bitcast(I32)
@@ -94,11 +112,14 @@ def tile_list_tablora_tm_none_kernel(tc, tab, w4_words, w4_scales, down, up, off
             )
 
         def load_w4(i):
-            a0, a1, first, width = W4LOADS[i]
-            nc.sync.dma_start(
-                out=w4_sb[i][:].bitcast(I32).rearrange("p (a c) -> p a c", a=a1 - a0),
-                in_=w4_i[a0:a1, :, first // 2 : (first + width) // 2].rearrange("a p c -> p a c"),
-            )
+            (a0, h0), (a1, h1) = W4LOADS[i]
+            if h0 == h1:
+                src = w4_i[a0 : a1 + 1 : a1 - a0, :, 256 * h0 : 256 * (h0 + 1)].rearrange("k p c -> p k c")
+            else:
+                r0, r1 = 2 * P * a0 + h0, 2 * P * a1 + h1
+                rows = w4_i.rearrange("a p (h c) -> (a p h) c", h=2)[r0 : 2 * r1 - r0]
+                src = rows.rearrange("(k r) c -> r k c", k=2)[0 : 2 * P - 1 : 2]
+            nc.sync.dma_start(out=w4_sb[i][:].bitcast(I32).rearrange("p (k c) -> p k c", k=2), in_=src)
 
         def load_up(g):
             first, width = PIECES[g]
@@ -202,53 +223,45 @@ def tile_list_tablora_tm_none_kernel(tc, tab, w4_words, w4_scales, down, up, off
                 in_=h_grp[j][:].rearrange("p n s -> p (n s)"),
             )
 
-        def multiply_w4(a, g, halves=(0, 1), stop=False):
-            first, width, tags = SUMS[g]
+        def multiply_w4(a, b):
+            tag, halves, first, width = BANKS[b]
             step = BANK if width == BANK else P
             for j in halves:
                 js = slice(P * j, P * (j + 1))
-                tag, acc = bank(g, j)
-                for n in range(0, width, step):
-                    col = first + n
-                    i = [k for k, (a0, a1, f, w) in enumerate(W4LOADS) if a0 <= a < a1 and f <= col < f + w][0]
-                    a0, a1, f, w = W4LOADS[i]
-                    at = (a - a0) * w + col - f
-                    nc.tensor.matmul_mx(
-                        out=acc[:, n : n + step],
-                        lhsT=v_codes[a][:, js].bitcast(FP8X4),
-                        lhsT_scale=v_planes[a][:, js],
-                        rhs=w4_sb[i][:, 2 * at : 2 * (at + step)].bitcast(FP4X4),
-                        rhs_scale=w4_plane[:, a * M + col : a * M + col + step],
-                        start=tag not in opened,
-                        stop=stop and n + step == width and (len(tags) == 2 or j == 1),
+                for col in range(first, first + width, step):
+                    piece = (a, col // BANK)
+                    i = [k for k, pieces in enumerate(W4LOADS) if piece in pieces][0]
+                    at = W4LOADS[i].index(piece) * BANK + col % BANK
+                    accumulate(
+                        b,
+                        j,
+                        col,
+                        step,
+                        v_codes[a][:, js].bitcast(FP8X4),
+                        v_planes[a][:, js],
+                        w4_sb[i][:, 2 * at : 2 * (at + step)].bitcast(FP4X4),
+                        w4_plane[:, a * M + col : a * M + col + step],
                     )
-                    opened.add(tag)
 
-        def multiply_up(c, halves=(0, 1), stop=False):
+        def multiply_up(c, j):
             first, width, share = CHUNKS[c]
-            g = [k for k, (f, w, tags) in enumerate(SUMS) if f <= first < f + w][0]
-            at = first - SUMS[g][0]
-            for j in halves:
-                tag, acc = bank(g, j)
-                nc.tensor.matmul_mx(
-                    out=acc[:, at : at + width],
-                    lhsT=h_codes[j][:].bitcast(FP8X4),
-                    lhsT_scale=h_scales[j][:],
-                    rhs=u_codes[c][:].bitcast(FP8X4),
-                    rhs_scale=u_scales[c][:],
-                    start=tag not in opened,
-                    stop=stop and (len(SUMS[g][2]) == 2 or j == 1),
-                )
-                opened.add(tag)
+            b = [k for k, (tag, halves, f, w) in enumerate(BANKS) if j in halves and f <= first < f + w][0]
+            accumulate(
+                b,
+                j,
+                first,
+                width,
+                h_codes[j][:].bitcast(FP8X4),
+                h_scales[j][:],
+                u_codes[c][:].bitcast(FP8X4),
+                u_scales[c][:],
+            )
 
-        def empty(g, j, engine):
-            first, width, tags = SUMS[g]
+        def empty(b, j, engine):
+            tag, halves, first, width = BANKS[b]
             k = [k for k, (f, w) in enumerate(STORES) if f <= first < f + w][0]
             at = first - STORES[k][0]
-            if len(tags) == 2:
-                dst, src = o_sb[k][:, j, at : at + width], bank(g, j)[1]
-            else:
-                dst, src = o_sb[k][:, :, at : at + width], o_ps[tags[0]][:].rearrange("p (j n) -> p j n", j=2)
+            dst, src = o_sb[k][:, j, at : at + width], o_ps[b][:, halves.index(j), :]
             if engine == "s":
                 nc.scalar.copy(out=dst, in_=src)
             else:
@@ -277,8 +290,8 @@ def tile_list_tablora_tm_none_kernel(tc, tab, w4_words, w4_scales, down, up, off
         load_w4(0)
         load_up(0)
         load_w4(1)
-        load_w4(2)
         load_up(1)
+        load_w4(2)
         load_up(2)
         round_down(0)
         quantize_down(0)
@@ -297,47 +310,51 @@ def tile_list_tablora_tm_none_kernel(tc, tab, w4_words, w4_scales, down, up, off
         empty_h(1, "v")
         quantize_h(0)
         quantize_h(1)
-        multiply_w4(0, 0)
-        multiply_w4(0, 1)
-        multiply_w4(0, 2)
-        multiply_w4(0, 3)
+        for a in range(PASSES):
+            for b in range(3):
+                multiply_w4(a, b)
         round_up(0)
         round_up(1)
-        multiply_w4(1, 0)
         quantize_up(0)
         quantize_up(1)
-        multiply_w4(2, 0, (0,))
-        multiply_up(0, (0,))
-        multiply_up(1, (0,), stop=True)
-        multiply_w4(2, 0, (1,))
-        multiply_up(0, (1,))
-        multiply_up(1, (1,), stop=True)
+        multiply_up(0, 0)
+        multiply_up(0, 1)
+        multiply_up(1, 0)
+        multiply_up(1, 1)
         empty(0, 0, "s")
+        empty(1, 0, "s")
         store(0, 0, "y")
-        empty(0, 1, "s")
+        empty(2, 1, "s")
         store(0, 1, "y")
-        multiply_w4(1, 1)
-        multiply_w4(2, 1)
+        for b in range(3, 8):
+            multiply_w4(1, b)
         round_up(2)
         quantize_up(2)
-        multiply_up(2, stop=True)
-        multiply_w4(1, 2)
-        multiply_w4(2, 2)
-        multiply_w4(1, 3)
-        multiply_w4(2, 3)
+        for a in (0, 2):
+            multiply_w4(a, 3)
+        multiply_up(2, 0)
+        multiply_up(2, 1)
+        for b in range(4, 6):
+            for a in (0, 2):
+                multiply_w4(a, b)
         round_up(3)
         round_up(4)
         quantize_up(3)
-        multiply_up(3, stop=True)
+        multiply_up(3, 0)
+        multiply_up(3, 1)
+        for b in range(6, 8):
+            for a in (0, 2):
+                multiply_w4(a, b)
         quantize_up(4)
-        empty(1, 0, "s")
-        store(1, 0, "y")
-        empty(1, 1, "s")
-        store(1, 1, "y")
-        multiply_up(4, stop=True)
-        empty(2, 0, "s")
-        empty(2, 1, "v")
-        store(2, 2, "y")
         empty(3, 0, "s")
-        empty(3, 1, "v")
+        store(1, 0, "y")
+        empty(3, 1, "s")
+        store(1, 1, "y")
+        multiply_up(4, 0)
+        multiply_up(4, 1)
+        empty(4, 0, "s")
+        empty(5, 1, "v")
+        store(2, 2, "y")
+        empty(6, 0, "s")
+        empty(7, 1, "v")
         store(3, 2, "y")

@@ -38,7 +38,7 @@ BANKS = (
     ("h1", (1,), 896, 128),
 )
 STORES = ((0, 512), (512, 256), (768, 128), (896, 128))
-W4LOADS = (((0, 0), (1, 0)), ((1, 1), (2, 0)), ((0, 1), (2, 1)))
+W4LOADS = ((0, 2, 0, 512), (2, 3, 0, 1024), (0, 2, 512, 256), (0, 2, 768, 256))
 WORDLOADS = ((0, 1), (1, 2), (2, 3))
 DOWN_ON_VECTOR = (0, 0, 88)
 
@@ -57,7 +57,7 @@ def tile_list_tablora_tm_none_kernel(tc, tab, w4_words, w4_scales, down, up, off
         tab_rows = sbuf("tab_rows", [P, PASSES * T // 4], I32)
         picked_rows = sbuf("picked_rows", [P, PASSES * S], U8)
         plane = sbuf("plane", [P, W4_COLS + V_COLS], I32)
-        w4_sb = [sbuf(f"w4_sb{i}", [P, 2 * M], U8) for i in range(len(W4LOADS))]
+        w4_sb = [sbuf(f"w4_sb{i}", [P, (a1 - a0) * 2 * width], U8) for i, (a0, a1, first, width) in enumerate(W4LOADS)]
         d_raw = [sbuf(f"d_raw{a}", [P, 4, R], F32) for a in range(PASSES)]
         d_grp = [sbuf(f"d_grp{a}", [P, 4, P, 4], BF16) for a in range(PASSES)]
         d_codes = [sbuf(f"d_codes{a}", [P, R], U32) for a in range(PASSES)]
@@ -112,14 +112,11 @@ def tile_list_tablora_tm_none_kernel(tc, tab, w4_words, w4_scales, down, up, off
             )
 
         def load_w4(i):
-            (a0, h0), (a1, h1) = W4LOADS[i]
-            if h0 == h1:
-                src = w4_i[a0 : a1 + 1 : a1 - a0, :, 256 * h0 : 256 * (h0 + 1)].rearrange("k p c -> p k c")
-            else:
-                r0, r1 = 2 * P * a0 + h0, 2 * P * a1 + h1
-                rows = w4_i.rearrange("a p (h c) -> (a p h) c", h=2)[r0 : 2 * r1 - r0]
-                src = rows.rearrange("(k r) c -> r k c", k=2)[0 : 2 * P - 1 : 2]
-            nc.sync.dma_start(out=w4_sb[i][:].bitcast(I32).rearrange("p (k c) -> p k c", k=2), in_=src)
+            a0, a1, first, width = W4LOADS[i]
+            nc.sync.dma_start(
+                out=w4_sb[i][:].bitcast(I32).rearrange("p (a c) -> p a c", a=a1 - a0),
+                in_=w4_i[a0:a1, :, first // 2 : (first + width) // 2].rearrange("a p c -> p a c"),
+            )
 
         def load_up(g):
             first, width = PIECES[g]
@@ -149,7 +146,14 @@ def tile_list_tablora_tm_none_kernel(tc, tab, w4_words, w4_scales, down, up, off
         def gather_words(a):
             i = [k for k, (a0, a1) in enumerate(WORDLOADS) if a0 <= a < a1][0]
             at = (a - WORDLOADS[i][0]) * T
-            nc.vector.tensor_copy(v_codes[a][:], words[i][:, at : at + T].bitcast(U32).indirect(offsets[:]))
+            window = words[i][:, at : at + T].bitcast(U32)
+            if a < PASSES - 1:
+                nc.vector.tensor_copy(v_codes[a][:], window.indirect(offsets[:]))
+            else:
+                for j in range(2):
+                    nc.vector.tensor_copy(
+                        v_codes[a][:, P * j : P * (j + 1)], window.indirect(offsets[:, 8 * j : 8 * (j + 1)])
+                    )
 
         def round_down(a):
             share = DOWN_ON_VECTOR[a]
@@ -229,9 +233,9 @@ def tile_list_tablora_tm_none_kernel(tc, tab, w4_words, w4_scales, down, up, off
             for j in halves:
                 js = slice(P * j, P * (j + 1))
                 for col in range(first, first + width, step):
-                    piece = (a, col // BANK)
-                    i = [k for k, pieces in enumerate(W4LOADS) if piece in pieces][0]
-                    at = W4LOADS[i].index(piece) * BANK + col % BANK
+                    i = [k for k, (a0, a1, f, w) in enumerate(W4LOADS) if a0 <= a < a1 and f <= col < f + w][0]
+                    a0, a1, f, w = W4LOADS[i]
+                    at = (a - a0) * w + col - f
                     accumulate(
                         b,
                         j,
@@ -261,7 +265,10 @@ def tile_list_tablora_tm_none_kernel(tc, tab, w4_words, w4_scales, down, up, off
             tag, halves, first, width = BANKS[b]
             k = [k for k, (f, w) in enumerate(STORES) if f <= first < f + w][0]
             at = first - STORES[k][0]
-            dst, src = o_sb[k][:, j, at : at + width], o_ps[b][:, halves.index(j), :]
+            if j < 2:
+                dst, src = o_sb[k][:, j, at : at + width], o_ps[b][:, halves.index(j), :]
+            else:
+                dst, src = o_sb[k][:, :, at : at + width], o_ps[b][:]
             if engine == "s":
                 nc.scalar.copy(out=dst, in_=src)
             else:
@@ -293,6 +300,7 @@ def tile_list_tablora_tm_none_kernel(tc, tab, w4_words, w4_scales, down, up, off
         load_up(1)
         load_w4(2)
         load_up(2)
+        load_w4(3)
         round_down(0)
         quantize_down(0)
         gather_words(0)
@@ -310,13 +318,15 @@ def tile_list_tablora_tm_none_kernel(tc, tab, w4_words, w4_scales, down, up, off
         empty_h(1, "v")
         quantize_h(0)
         quantize_h(1)
-        for a in range(PASSES):
+        for a in range(2):
             for b in range(3):
                 multiply_w4(a, b)
         round_up(0)
         round_up(1)
         quantize_up(0)
         quantize_up(1)
+        for b in range(3):
+            multiply_w4(2, b)
         multiply_up(0, 0)
         multiply_up(0, 1)
         multiply_up(1, 0)
@@ -326,30 +336,25 @@ def tile_list_tablora_tm_none_kernel(tc, tab, w4_words, w4_scales, down, up, off
         store(0, 0, "y")
         empty(2, 1, "s")
         store(0, 1, "y")
-        for b in range(3, 8):
-            multiply_w4(1, b)
         round_up(2)
         quantize_up(2)
-        for a in (0, 2):
+        for a in (2, 0, 1):
             multiply_w4(a, 3)
         multiply_up(2, 0)
         multiply_up(2, 1)
-        for b in range(4, 6):
-            for a in (0, 2):
-                multiply_w4(a, b)
+        for b in range(4, 8):
+            multiply_w4(2, b)
         round_up(3)
         round_up(4)
         quantize_up(3)
+        quantize_up(4)
+        empty(3, 2, "s")
+        store(1, 2, "y")
+        for b in range(4, 8):
+            for a in range(2):
+                multiply_w4(a, b)
         multiply_up(3, 0)
         multiply_up(3, 1)
-        for b in range(6, 8):
-            for a in (0, 2):
-                multiply_w4(a, b)
-        quantize_up(4)
-        empty(3, 0, "s")
-        store(1, 0, "y")
-        empty(3, 1, "s")
-        store(1, 1, "y")
         multiply_up(4, 0)
         multiply_up(4, 1)
         empty(4, 0, "s")

@@ -25,22 +25,24 @@ V_COLS = PASSES * S // 4
 ROW0, STEP = 0, 8
 STAGED = slice(ROW0, ROW0 + STEP * (BLOCKS - 1) + 1, STEP)
 
-PIECES = ((0, 512), (512, 256), (768, 256))
-CHUNKS = ((0, 256, 160), (256, 256, 160), (512, 256, 256), (768, 128, 128), (896, 128, 128))
+DOWNLOADS = ((0, 1), (1, 2), (2, 3))
+WORDLOADS = ((0, 1), (1, 2), (2, 3))
+W4LOADS = ((0, 3, 0, 768), (0, 3, 768, 256))
+PIECES = ((0, 384), (384, 384), (768, 256))
+CHUNKS = ((0, 256, 160), (256, 128, 96), (384, 256, 160), (640, 128, 96), (768, 128, 128), (896, 128, 128))
 BANKS = (
-    ("a", (0,), 0, 256),
-    ("b", (0,), 256, 256),
-    ("c", (1,), 0, 512),
-    ("d", (0, 1), 512, 256),
+    ("a", (0,), 0, 384),
+    ("b", (1,), 0, 384),
+    ("c", (0,), 384, 384),
+    ("d", (1,), 384, 384),
     ("e", (0,), 768, 128),
     ("f", (1,), 768, 128),
     ("h0", (0,), 896, 128),
     ("h1", (1,), 896, 128),
 )
-STORES = ((0, 512), (512, 256), (768, 128), (896, 128))
-W4LOADS = ((0, 2, 0, 512), (2, 3, 0, 1024), (0, 2, 512, 256), (0, 2, 768, 256))
-WORDLOADS = ((0, 1), (1, 2), (2, 3))
+STORES = ((0, 384), (384, 384), (768, 128), (896, 128))
 DOWN_ON_VECTOR = (0, 0, 88)
+O_TAGS = ("u_raw1", "o_sb1", "o_sb2", "o_sb3")
 
 
 def tile_list_tablora_tm_none_kernel(tc, tab, w4_words, w4_scales, down, up, offs, out):
@@ -58,7 +60,7 @@ def tile_list_tablora_tm_none_kernel(tc, tab, w4_words, w4_scales, down, up, off
         picked_rows = sbuf("picked_rows", [P, PASSES * S], U8)
         plane = sbuf("plane", [P, W4_COLS + V_COLS], I32)
         w4_sb = [sbuf(f"w4_sb{i}", [P, (a1 - a0) * 2 * width], U8) for i, (a0, a1, first, width) in enumerate(W4LOADS)]
-        d_raw = [sbuf(f"d_raw{a}", [P, 4, R], F32) for a in range(PASSES)]
+        d_raw = [sbuf(f"d_raw{i}", [P, (a1 - a0) * 4, R], F32) for i, (a0, a1) in enumerate(DOWNLOADS)]
         d_grp = [sbuf(f"d_grp{a}", [P, 4, P, 4], BF16) for a in range(PASSES)]
         d_codes = [sbuf(f"d_codes{a}", [P, R], U32) for a in range(PASSES)]
         d_scales = [sbuf(f"d_scales{a}", [P, R], U8) for a in range(PASSES)]
@@ -70,7 +72,7 @@ def tile_list_tablora_tm_none_kernel(tc, tab, w4_words, w4_scales, down, up, off
         h_grp = [sbuf(f"h_grp{j}", [P, P, 4], BF16) for j in range(2)]
         h_codes = [sbuf(f"h_codes{j}", [P, P], U32) for j in range(2)]
         h_scales = [sbuf(f"h_scales{j}", [P, P], U8) for j in range(2)]
-        o_sb = [sbuf(f"o_sb{g}", [P, 2, width], F32) for g, (first, width) in enumerate(STORES)]
+        o_sb = {}
         h_ps = [psum.tile([P, 4, P], F32, name=f"h_ps{j}", tag=f"h{j}") for j in range(2)]
         o_ps = {}
         summed = {}
@@ -99,9 +101,11 @@ def tile_list_tablora_tm_none_kernel(tc, tab, w4_words, w4_scales, down, up, off
         w4_plane = plane[:, :W4_COLS].bitcast(U8)
         v_planes = [plane[:, W4_COLS:].bitcast(U8)[:, S * a : S * (a + 1)] for a in range(PASSES)]
 
-        def load_down(a):
+        def load_down(i):
+            a0, a1 = DOWNLOADS[i]
             nc.sync.dma_start(
-                out=d_raw[a][:], in_=down[512 * a : 512 * (a + 1), :].rearrange("(p t) r -> p t r", t=4)
+                out=d_raw[i][:].rearrange("p (a t) r -> p a (t r)", t=4),
+                in_=down[512 * a0 : 512 * a1, :].rearrange("(a p t) r -> p a (t r)", p=P, t=4),
             )
 
         def load_words(i):
@@ -157,11 +161,14 @@ def tile_list_tablora_tm_none_kernel(tc, tab, w4_words, w4_scales, down, up, off
 
         def round_down(a):
             share = DOWN_ON_VECTOR[a]
-            src = d_raw[a][:].rearrange("p t (m u e) -> p u m t e", u=2, e=2)
+            i = [k for k, (a0, a1) in enumerate(DOWNLOADS) if a0 <= a < a1][0]
+            at = 4 * (a - DOWNLOADS[i][0])
+            src = d_raw[i][:, at : at + 4, :].rearrange("p t (m u e) -> p u m t e", u=2, e=2)
             dst = d_grp[a][:].rearrange("p (u e) m t -> p u m t e", e=2)
             if share > 0:
                 nc.vector.tensor_copy(out=dst[:, :, :share], in_=src[:, :, :share])
-            nc.scalar.copy(out=dst[:, :, share:], in_=src[:, :, share:])
+            if share < P:
+                nc.scalar.copy(out=dst[:, :, share:], in_=src[:, :, share:])
 
         def quantize_down(a):
             nc.vector.quantize_mx(
@@ -265,6 +272,8 @@ def tile_list_tablora_tm_none_kernel(tc, tab, w4_words, w4_scales, down, up, off
             tag, halves, first, width = BANKS[b]
             k = [k for k, (f, w) in enumerate(STORES) if f <= first < f + w][0]
             at = first - STORES[k][0]
+            if k not in o_sb:
+                o_sb[k] = keep.tile([P, 2, STORES[k][1]], F32, name=f"o_sb{k}", tag=O_TAGS[k], align_bytes=1024)
             if j < 2:
                 dst, src = o_sb[k][:, j, at : at + width], o_ps[b][:, halves.index(j), :]
             else:
@@ -295,12 +304,9 @@ def tile_list_tablora_tm_none_kernel(tc, tab, w4_words, w4_scales, down, up, off
         load_words(1)
         load_words(2)
         load_w4(0)
-        load_up(0)
+        for g in range(3):
+            load_up(g)
         load_w4(1)
-        load_up(1)
-        load_w4(2)
-        load_up(2)
-        load_w4(3)
         round_down(0)
         quantize_down(0)
         gather_words(0)
@@ -310,56 +316,41 @@ def tile_list_tablora_tm_none_kernel(tc, tab, w4_words, w4_scales, down, up, off
         multiply_down(0)
         round_down(2)
         quantize_down(2)
-        gather_words(1)
-        multiply_down(1)
-        gather_words(2)
-        multiply_down(2)
+        for a in (1, 2):
+            gather_words(a)
+            multiply_down(a)
         empty_h(0, "s")
         empty_h(1, "v")
         quantize_h(0)
         quantize_h(1)
-        for a in range(2):
-            for b in range(3):
+        for b in range(4):
+            for a in range(PASSES):
                 multiply_w4(a, b)
-        round_up(0)
-        round_up(1)
-        quantize_up(0)
-        quantize_up(1)
-        for b in range(3):
-            multiply_w4(2, b)
-        multiply_up(0, 0)
-        multiply_up(0, 1)
-        multiply_up(1, 0)
-        multiply_up(1, 1)
-        empty(0, 0, "s")
-        empty(1, 0, "s")
-        store(0, 0, "y")
-        empty(2, 1, "s")
-        store(0, 1, "y")
-        round_up(2)
-        quantize_up(2)
-        for a in (2, 0, 1):
-            multiply_w4(a, 3)
-        multiply_up(2, 0)
-        multiply_up(2, 1)
-        for b in range(4, 8):
-            multiply_w4(2, b)
-        round_up(3)
+        for g in range(2):
+            round_up(2 * g)
+            round_up(2 * g + 1)
+            quantize_up(2 * g)
+            quantize_up(2 * g + 1)
+            for j in range(2):
+                multiply_up(2 * g, j)
+                multiply_up(2 * g + 1, j)
         round_up(4)
-        quantize_up(3)
+        round_up(5)
         quantize_up(4)
-        empty(3, 2, "s")
-        store(1, 2, "y")
-        for b in range(4, 8):
-            for a in range(2):
-                multiply_w4(a, b)
-        multiply_up(3, 0)
-        multiply_up(3, 1)
-        multiply_up(4, 0)
-        multiply_up(4, 1)
-        empty(4, 0, "s")
-        empty(5, 1, "v")
-        store(2, 2, "y")
-        empty(6, 0, "s")
-        empty(7, 1, "v")
-        store(3, 2, "y")
+        quantize_up(5)
+        empty(0, 0, "s")
+        store(0, 0, "y")
+        empty(1, 1, "s")
+        store(0, 1, "y")
+        for j in range(2):
+            empty(2 + j, j, "s")
+            store(1, j, "y")
+        for c in (4, 5):
+            for b in (2 * c - 4, 2 * c - 3):
+                for a in range(PASSES):
+                    multiply_w4(a, b)
+            multiply_up(c, 0)
+            multiply_up(c, 1)
+            empty(2 * c - 4, 0, "s")
+            empty(2 * c - 3, 1, "v")
+            store(c - 2, 2, "y")

from contextlib import ExitStack

import concourse.mybir as mybir

K, R, M, T, S = 1536, 512, 1024, 1024, 256
FLOPS = 2 * S * (K * R + K * M + R * M)

F32 = mybir.dt.float32
BF16 = mybir.dt.bfloat16
I32 = mybir.dt.int32
U32 = mybir.dt.uint32
U16 = mybir.dt.uint16
U8 = mybir.dt.uint8
FP8X4 = mybir.dt.float8_e4m3fn_x4
FP4X4 = mybir.dt.float4_e2m1fn_x4

P = 128
PASSES = K // 512
BLOCKS = 16
BANK = 512
WORD_COLS = 512 * T // 4
W4_COLS = PASSES * M // 4
V_COLS = PASSES * S // 4

ROW0, STEP = 0, 8
STAGED = slice(ROW0, ROW0 + STEP * (BLOCKS - 1) + 1, STEP)

DOWNLOADS = ((0, 1), (1, 2), (2, 3))
WORDLOADS = ((0, 1), (1, 2), (2, 3))
W4LOADS = ((0, 3, 0, 768), (0, 3, 768, 256))
PIECES = ((0, 384), (384, 384), (768, 256))
CHUNKS = ((0, 256, 160), (256, 128, 96), (384, 256, 160), (640, 128, 96), (768, 128, 128), (896, 128, 128))
BANKS = (
    ("a", (0,), 0, 384),
    ("b", (1,), 0, 384),
    ("c", (0,), 384, 384),
    ("d", (1,), 384, 384),
    ("e", (0,), 768, 128),
    ("f", (1,), 768, 128),
    ("h0", (0,), 896, 128),
    ("h1", (1,), 896, 128),
)
STORES = ((0, 384), (384, 384), (768, 128), (896, 128))
DOWN_ON_VECTOR = (0, 0, 88)
O_TAGS = ("u_raw1", "o_sb1", "o_sb2", "o_sb3")


def tile_list_tablora_tm_none_kernel(tc, tab, w4_words, w4_scales, down, up, offs, out):
    nc = tc.nc
    with ExitStack() as ctx:
        keep = ctx.enter_context(tc.tile_pool(name="keep", bufs=1))
        psum = ctx.enter_context(tc.psum_pool(name="psum", bufs=1))

        def sbuf(name, shape, dtype):
            return keep.tile(shape, dtype, name=name, align_bytes=1024)

        offsets = keep.tile([P, S // 16], U16, name="offsets")
        words = [sbuf(f"words{i}", [P, (a1 - a0) * T], I32) for i, (a0, a1) in enumerate(WORDLOADS)]
        tab_rows = sbuf("tab_rows", [P, PASSES * T // 4], I32)
        picked_rows = sbuf("picked_rows", [P, PASSES * S], U8)
        plane = sbuf("plane", [P, W4_COLS + V_COLS], I32)
        w4_sb = [sbuf(f"w4_sb{i}", [P, (a1 - a0) * 2 * width], U8) for i, (a0, a1, first, width) in enumerate(W4LOADS)]
        d_raw = [sbuf(f"d_raw{i}", [P, (a1 - a0) * 4, R], F32) for i, (a0, a1) in enumerate(DOWNLOADS)]
        d_grp = [sbuf(f"d_grp{a}", [P, 4, P, 4], BF16) for a in range(PASSES)]
        d_codes = [sbuf(f"d_codes{a}", [P, R], U32) for a in range(PASSES)]
        d_scales = [sbuf(f"d_scales{a}", [P, R], U8) for a in range(PASSES)]
        u_raw = [sbuf(f"u_raw{g}", [P, 4, width], F32) for g, (first, width) in enumerate(PIECES)]
        u_grp = [sbuf(f"u_grp{c}", [P, width, 4], BF16) for c, (first, width, share) in enumerate(CHUNKS)]
        u_codes = [sbuf(f"u_codes{c}", [P, width], U32) for c, (first, width, share) in enumerate(CHUNKS)]
        u_scales = [sbuf(f"u_scales{c}", [P, width], U8) for c, (first, width, share) in enumerate(CHUNKS)]
        v_codes = [sbuf(f"v_codes{a}", [P, S], U32) for a in range(PASSES)]
        h_grp = [sbuf(f"h_grp{j}", [P, P, 4], BF16) for j in range(2)]
        h_codes = [sbuf(f"h_codes{j}", [P, P], U32) for j in range(2)]
        h_scales = [sbuf(f"h_scales{j}", [P, P], U8) for j in range(2)]
        o_sb = {}
        h_ps = [psum.tile([P, 4, P], F32, name=f"h_ps{j}", tag=f"h{j}") for j in range(2)]
        o_ps = {}
        summed = {}

        def accumulate(b, j, col, n, lhsT, lhsT_scale, rhs, rhs_scale):
            tag, halves, first, width = BANKS[b]
            if b not in o_ps:
                o_ps[b] = psum.tile([P, len(halves), width], F32, name=f"o_ps{b}", tag=tag)
                summed[b] = 0
            start = summed[b] == 0
            summed[b] = summed[b] + n
            nc.tensor.matmul_mx(
                out=o_ps[b][:, halves.index(j), col - first : col - first + n],
                lhsT=lhsT,
                lhsT_scale=lhsT_scale,
                rhs=rhs,
                rhs_scale=rhs_scale,
                start=start,
                stop=summed[b] == (PASSES + 1) * len(halves) * width,
            )

        tab_i = tab.bitcast(I32)
        w4_i = w4_words.bitcast(I32)
        up_v = up.rearrange("(p t) n -> p t n", t=4)
        out_v = out.rearrange("(j p) n -> p j n", j=2)
        w4_plane = plane[:, :W4_COLS].bitcast(U8)
        v_planes = [plane[:, W4_COLS:].bitcast(U8)[:, S * a : S * (a + 1)] for a in range(PASSES)]

        def load_down(i):
            a0, a1 = DOWNLOADS[i]
            nc.sync.dma_start(
                out=d_raw[i][:].rearrange("p (a t) r -> p a (t r)", t=4),
                in_=down[512 * a0 : 512 * a1, :].rearrange("(a p t) r -> p a (t r)", p=P, t=4),
            )

        def load_words(i):
            a0, a1 = WORDLOADS[i]
            nc.sync.dma_start(
                out=words[i][:].rearrange("p (a c) -> p a c", c=T),
                in_=tab_i[a0:a1, :WORD_COLS].rearrange("a (p c) -> p a c", p=P),
            )

        def load_w4(i):
            a0, a1, first, width = W4LOADS[i]
            nc.sync.dma_start(
                out=w4_sb[i][:].bitcast(I32).rearrange("p (a c) -> p a c", a=a1 - a0),
                in_=w4_i[a0:a1, :, first // 2 : (first + width) // 2].rearrange("a p c -> p a c"),
            )

        def load_up(g):
            first, width = PIECES[g]
            nc.sync.dma_start(out=u_raw[g][:], in_=up_v[:, :, first : first + width])

        def stage_scales():
            nc.sync.dma_start(
                out=tab_rows[STAGED, :].rearrange("q (a c) -> q a c", a=PASSES),
                in_=tab_i[:, WORD_COLS:].rearrange("a (q c) -> q a c", q=BLOCKS),
            )
            nc.sync.dma_start(
                out=plane[STAGED, :W4_COLS].rearrange("q (a c) -> q a c", a=PASSES),
                in_=w4_scales.bitcast(I32).rearrange("a q c -> q a c"),
            )
            tab_bytes = tab_rows[:].bitcast(U8)
            for a in range(PASSES):
                nc.vector.tensor_copy(
                    picked_rows[:, S * a : S * (a + 1)], tab_bytes[:, T * a : T * (a + 1)].indirect(offsets[:])
                )
            nc.vector.tensor_copy(out=plane[:, W4_COLS:], in_=picked_rows[:].bitcast(I32))

        def carry_scales():
            for i in range(1, 4):
                rows = slice(ROW0 + STEP * i, ROW0 + STEP * (i + 12) + 1, 4 * STEP)
                nc.sync.dma_start(out=plane[i:P:32, :], in_=plane[rows, :])

        def gather_words(a):
            i = [k for k, (a0, a1) in enumerate(WORDLOADS) if a0 <= a < a1][0]
            at = (a - WORDLOADS[i][0]) * T
            window = words[i][:, at : at + T].bitcast(U32)
            if a < PASSES - 1:
                nc.vector.tensor_copy(v_codes[a][:], window.indirect(offsets[:]))
            else:
                for j in range(2):
                    nc.vector.tensor_copy(
                        v_codes[a][:, P * j : P * (j + 1)], window.indirect(offsets[:, 8 * j : 8 * (j + 1)])
                    )

        def round_down(a):
            share = DOWN_ON_VECTOR[a]
            i = [k for k, (a0, a1) in enumerate(DOWNLOADS) if a0 <= a < a1][0]
            at = 4 * (a - DOWNLOADS[i][0])
            src = d_raw[i][:, at : at + 4, :].rearrange("p t (m u e) -> p u m t e", u=2, e=2)
            dst = d_grp[a][:].rearrange("p (u e) m t -> p u m t e", e=2)
            if share > 0:
                nc.vector.tensor_copy(out=dst[:, :, :share], in_=src[:, :, :share])
            if share < P:
                nc.scalar.copy(out=dst[:, :, share:], in_=src[:, :, share:])

        def quantize_down(a):
            nc.vector.quantize_mx(
                out=d_codes[a][:].bitcast(FP8X4),
                scales=d_scales[a][:],
                in_=d_grp[a][:].rearrange("p s m t -> p (s m t)"),
            )

        def round_up(c, engines="vs"):
            first, width, share = CHUNKS[c]
            g = [k for k, (f, w) in enumerate(PIECES) if f <= first < f + w][0]
            at = first - PIECES[g][0]
            src = u_raw[g][:, :, at : at + width].rearrange("p t (b i) -> p b t i", i=4)
            dst = u_grp[c][:].rearrange("p (b i) t -> p b t i", i=4)
            if share > 0 and "v" in engines:
                nc.vector.tensor_copy(out=dst[:, : share // 4], in_=src[:, : share // 4])
            if share < width and "s" in engines:
                nc.scalar.copy(out=dst[:, share // 4 :], in_=src[:, share // 4 :])

        def quantize_up(c):
            nc.vector.quantize_mx(
                out=u_codes[c][:].bitcast(FP8X4), scales=u_scales[c][:], in_=u_grp[c][:].rearrange("p n t -> p (n t)")
            )

        def multiply_down(a):
            for j in range(2):
                js = slice(P * j, P * (j + 1))
                for s in range(4):
                    ss = slice(P * s, P * (s + 1))
                    nc.tensor.matmul_mx(
                        out=h_ps[j][:, s, :],
                        lhsT=d_codes[a][:, ss].bitcast(FP8X4),
                        lhsT_scale=d_scales[a][:, ss],
                        rhs=v_codes[a][:, js].bitcast(FP8X4),
                        rhs_scale=v_planes[a][:, js],
                        start=(a == 0 and s == 0),
                        stop=(a == PASSES - 1 and s == 3),
                    )

        def warm_tensor(a):
            unread = psum.tile([P, BANK], F32, name="unread", tag="e")
            for repeat in range(2):
                nc.tensor.matmul_mx(
                    out=unread[:],
                    lhsT=d_codes[a][:, :P].bitcast(FP8X4),
                    lhsT_scale=d_scales[a][:, :P],
                    rhs=d_codes[a][:].bitcast(FP8X4),
                    rhs_scale=d_scales[a][:],
                    start=True,
                    stop=True,
                )

        def empty_h(j, engine):
            if engine == "s":
                nc.scalar.copy(out=h_grp[j][:], in_=h_ps[j][:].rearrange("p s n -> p n s"))
            else:
                nc.vector.tensor_copy(out=h_grp[j][:], in_=h_ps[j][:].rearrange("p s n -> p n s"))

        def quantize_h(j):
            nc.vector.quantize_mx(
                out=h_codes[j][:].bitcast(FP8X4),
                scales=h_scales[j][:],
                in_=h_grp[j][:].rearrange("p n s -> p (n s)"),
            )

        def multiply_w4(a, b):
            tag, halves, first, width = BANKS[b]
            step = BANK if width == BANK else P
            for j in halves:
                js = slice(P * j, P * (j + 1))
                for col in range(first, first + width, step):
                    i = [k for k, (a0, a1, f, w) in enumerate(W4LOADS) if a0 <= a < a1 and f <= col < f + w][0]
                    a0, a1, f, w = W4LOADS[i]
                    at = (a - a0) * w + col - f
                    accumulate(
                        b,
                        j,
                        col,
                        step,
                        v_codes[a][:, js].bitcast(FP8X4),
                        v_planes[a][:, js],
                        w4_sb[i][:, 2 * at : 2 * (at + step)].bitcast(FP4X4),
                        w4_plane[:, a * M + col : a * M + col + step],
                    )

        def multiply_up(c, j):
            first, width, share = CHUNKS[c]
            b = [k for k, (tag, halves, f, w) in enumerate(BANKS) if j in halves and f <= first < f + w][0]
            accumulate(
                b,
                j,
                first,
                width,
                h_codes[j][:].bitcast(FP8X4),
                h_scales[j][:],
                u_codes[c][:].bitcast(FP8X4),
                u_scales[c][:],
            )

        def empty(b, j, engine):
            tag, halves, first, width = BANKS[b]
            k = [k for k, (f, w) in enumerate(STORES) if f <= first < f + w][0]
            at = first - STORES[k][0]
            if k not in o_sb:
                o_sb[k] = keep.tile([P, 2, STORES[k][1]], F32, name=f"o_sb{k}", tag=O_TAGS[k], align_bytes=1024)
            if j < 2:
                dst, src = o_sb[k][:, j, at : at + width], o_ps[b][:, halves.index(j), :]
            else:
                dst, src = o_sb[k][:, :, at : at + width], o_ps[b][:]
            if engine == "s":
                nc.scalar.copy(out=dst, in_=src)
            else:
                nc.vector.tensor_copy(out=dst, in_=src)

        def store(k, j, engine):
            first, width = STORES[k]
            queue = nc.scalar if engine == "s" else nc.sync
            if j < 2:
                queue.dma_start(out=out_v[:, j, first : first + width], in_=o_sb[k][:, j, :])
            else:
                queue.dma_start(out=out_v[:, :, first : first + width], in_=o_sb[k][:])

        nc.vector.memset(tab_rows[:], 0)
        nc.vector.memset(plane[:, :W4_COLS], 0)

        load_down(0)
        nc.sync.dma_start(offsets[:], offs)
        stage_scales()
        load_down(1)
        load_words(0)
        load_down(2)
        carry_scales()
        load_words(1)
        load_words(2)
        load_w4(0)
        for g in range(3):
            load_up(g)
        load_w4(1)
        round_down(0)
        quantize_down(0)
        gather_words(0)
        round_down(1)
        quantize_down(1)
        warm_tensor(1)
        multiply_down(0)
        round_down(2)
        quantize_down(2)
        for a in (1, 2):
            gather_words(a)
            multiply_down(a)
        empty_h(0, "s")
        empty_h(1, "v")
        quantize_h(0)
        quantize_h(1)
        for b in range(4):
            for a in range(PASSES):
                multiply_w4(a, b)
        for g in range(2):
            round_up(2 * g)
            round_up(2 * g + 1)
            quantize_up(2 * g)
            quantize_up(2 * g + 1)
            for j in range(2):
                multiply_up(2 * g, j)
                multiply_up(2 * g + 1, j)
        round_up(4)
        round_up(5)
        quantize_up(4)
        quantize_up(5)
        empty(0, 0, "s")
        store(0, 0, "y")
        empty(1, 1, "s")
        store(0, 1, "y")
        for j in range(2):
            empty(2 + j, j, "s")
            store(1, j, "y")
        for c in (4, 5):
            for b in (2 * c - 4, 2 * c - 3):
                for a in range(PASSES):
                    multiply_w4(a, b)
            multiply_up(c, 0)
            multiply_up(c, 1)
            empty(2 * c - 4, 0, "s")
            empty(2 * c - 3, 1, "v")
            store(c - 2, 2, "y")
